import numpy as np
import ml_dtypes


def mxq(x, axis, fmt="e4m3"):
    dtype, down = {"e4m3": (ml_dtypes.float8_e4m3fn, 7), "e5m2": (ml_dtypes.float8_e5m2, 14)}[fmt]
    v = np.moveaxis(np.asarray(x, np.float32).astype(ml_dtypes.bfloat16).astype(np.float64), axis, -1)
    blocks = v.reshape(v.shape[:-1] + (-1, 32))
    amax = np.abs(blocks).max(-1, keepdims=True)
    byte = np.maximum(np.where(amax > 0, np.frexp(amax)[1] - 1 + 127, 0) - down, 1)
    scale = np.exp2(byte - 127.0)
    codes = (blocks / scale).astype(np.float32).astype(dtype).astype(np.float64)
    return np.moveaxis((codes * scale).reshape(v.shape), -1, axis)


WIDE = False


def mx_kscale(k):
    if not WIDE:
        return np.ones(k)
    levels = np.array([10, -10, 5, -5, 0])
    if k % 512:
        return np.exp2(np.random.permutation(np.resize(levels, k // 32))).repeat(32)
    a = np.empty((k // 512, 16))
    for p in range(k // 512):
        a[p, :8] = np.random.permutation(np.resize(levels, 8))
        for g in range(8):
            far = levels[np.abs(levels - a[p, g]) >= 10]
            a[p, g + 8] = far[np.random.randint(len(far))]
    return np.exp2(a.ravel()).repeat(32)


BF16 = ml_dtypes.bfloat16


def bf(x):
    return np.asarray(x, np.float32).astype(BF16)


def f64(x):
    return np.asarray(x).astype(np.float64)


E2M1 = np.array([0.0, 0.5, 1.0, 1.5, 2.0, 3.0, 4.0, 6.0, -0.0, -0.5, -1.0, -1.5, -2.0, -3.0, -4.0, -6.0])


def pack_weight(w, fmt):
    k, n = w.shape
    w = f64(bf(w)).reshape(k // 32, 32, n)
    amax = np.abs(w).max(1)
    if fmt == "e4m3":
        byte = np.frexp(amax)[1] - 1 + 127 - 7
    else:
        mant, ex = np.frexp(amax / 6.0)
        byte = np.where(mant > 0.5, ex, ex - 1) + 127
    byte = np.clip(np.where(amax > 0, byte, 1), 1, 254)
    scaled = (w * np.exp2(127.0 - byte)[:, None, :]).reshape(k, n).astype(np.float32)
    by_word = np.ascontiguousarray(scaled.reshape(k // 512, 128, 4, n).transpose(0, 1, 3, 2))
    if fmt == "e4m3":
        words = by_word.astype(ml_dtypes.float8_e4m3fn).view(np.uint8)
    else:
        c = by_word.astype(ml_dtypes.float4_e2m1fn).view(np.uint8) & 0xF
        words = c[..., 0::2] | (c[..., 1::2] << 4)
    return np.ascontiguousarray(words), np.ascontiguousarray(byte.astype(np.uint8).reshape(k // 512, 16, n))


def unpack_weight(words, scales, fmt):
    g, p, n, _ = words.shape
    if fmt == "e4m3":
        vals = np.ascontiguousarray(words).view(ml_dtypes.float8_e4m3fn).astype(np.float64)
    else:
        nib = np.empty((g, p, n, 4), np.uint8)
        nib[..., 0::2] = words & 0xF
        nib[..., 1::2] = words >> 4
        vals = E2M1[nib]
    vals = vals * np.repeat(np.exp2(scales.astype(np.float64) - 127.0), 8, axis=1)[..., None]
    return vals.transpose(0, 1, 3, 2).reshape(g * 512, n)
def pack4(w):
    words, scales = pack_weight(w, "e2m1")
    return words.reshape(words.shape[0], 128, -1), scales


def unpack4(words, scales):
    return unpack_weight(words.reshape(words.shape[0], 128, -1, 2), scales, "e2m1")


def planes(Y):
    n, m = Y.shape
    b = f64(bf(Y)).reshape(n // 32, 32, m)
    amax = np.abs(b).max(1)
    byte = np.clip(np.where(amax > 0, np.frexp(amax)[1] - 1 + 127 - 7, 1), 1, 254)
    codes = (b * np.exp2(127.0 - byte)[:, None, :]).reshape(n, m).astype(np.float32).astype(ml_dtypes.float8_e4m3fn).view(np.uint8)
    words = codes.reshape(n // 512, 128, 4, m).transpose(0, 1, 3, 2)
    return np.ascontiguousarray(words), np.ascontiguousarray(byte.astype(np.uint8).reshape(n // 512, 16, m))


N, D, E = 1024, 1024, 1024


def setup_inputs():
    s = mx_kscale(E)
    u = mx_kscale(N)
    w = np.random.standard_normal((E, D)) / np.sqrt(E)
    gup = np.random.standard_normal((E, E)) * 8.0
    a = np.random.uniform(-np.pi, np.pi, (N, D))
    r = np.random.uniform(0.5, 1.5, N)
    c = np.random.uniform(0.25, 1.25, N)
    words, scales = pack4(w * s[:, None])
    return {"w_words": words, "w_scales": scales, "gup": bf(gup / s[:, None] / s[None, :]), "a": bf(a), "r": bf(r * u), "c": bf(c / (u * u))}


def _pull_through_linear(wq, gup):
    p = wq.T @ mxq(gup, 0, "e4m3")
    return mxq(p, 1, "e4m3") @ wq


def _sine_slope(a, r):
    return r[:, None] * np.cos(a)


def core(w_words, w_scales, gup, a, r, c):
    n = a.shape[0]
    q = _pull_through_linear(unpack4(w_words, w_scales), f64(gup))
    fp = _sine_slope(f64(a), f64(r))
    fc = f64(c)[:, None] * fp
    m = (mxq(fc, 0, "e4m3").T @ mxq(fp, 0, "e4m3")) / n
    hcur = q * m
    return hcur


def reference(w_words, w_scales, gup, a, r, c):
    R_out = core(w_words, w_scales, gup, a, r, c)
    words, scales = planes(R_out.T)
    return R_out, words, scales

@@ -1,0 +1,415 @@
+from contextlib import ExitStack
+
+import math
+
+import concourse.mybir as mybir
+from concourse.masks import make_identity
+
+F32 = mybir.dt.float32
+BF16 = mybir.dt.bfloat16
+U32 = mybir.dt.uint32
+I32 = mybir.dt.int32
+U8 = mybir.dt.uint8
+E4M3 = mybir.dt.float8_e4m3fn_x4
+E2M1 = mybir.dt.float4_e2m1fn_x4
+ALU = mybir.AluOpType
+ACT = mybir.ActivationFunctionType
+
+N = 1024
+FLOPS = 3 * 2 * N * N * N
+G = 2
+P = 128
+CH = 256
+NCH = 8
+
+
+def tile_kfrasinecurvaturepullback_x2_kernel(tc, w_words, w_scales, gup, a, r, c, out_0, out_1, out_2):
+    nc = tc.nc
+    with ExitStack() as ctx:
+        keep = ctx.enter_context(tc.tile_pool(name="keep", bufs=1))
+        stage = ctx.enter_context(tc.tile_pool(name="stage", bufs=3))
+        psum = ctx.enter_context(tc.psum_pool(name="psum", bufs=6))
+        psum_t = ctx.enter_context(tc.psum_pool(name="psum_t", bufs=2))
+        ctx.enter_context(tc.manual_schedule())
+
+        a_sb = keep.tile([P, G, 4, N], BF16, align_bytes=64, name="a_sb")
+        gup_sb = []
+        for g in range(G):
+            gup_half = keep.tile([P, 4, N], BF16, align_bytes=64, name="raw", bufs=2)
+            gup_sb.append(gup_half)
+        cos_sb = keep.tile([P, NCH, 4, CH], F32, align_bytes=64, name="cos_sb")
+        w_sb = keep.tile([P, G, 2 * N], U8, align_bytes=64, name="w_sb")
+        ws_sb = keep.tile([P, G, N], U8, align_bytes=64, name="ws_sb")
+        r_bf = keep.tile([P, G, 4], BF16, align_bytes=64, name="r_bf")
+        c_bf = keep.tile([P, G, 4], BF16, align_bytes=64, name="c_bf")
+        r_f = keep.tile([P, G * 4], F32, align_bytes=64, name="r_f")
+        cr_f = keep.tile([P, G * 4], F32, align_bytes=64, name="cr_f")
+        ident = keep.tile([P, P], F32, align_bytes=64, name="ident")
+        g_codes = keep.tile([P, G, N], U32, align_bytes=64, name="g_codes")
+        g_scales = keep.tile([P, G, N], U8, align_bytes=64, name="g_scales")
+        fp_codes = keep.tile([P, G, N], U32, align_bytes=64, name="fp_codes")
+        fp_scales = keep.tile([P, G, N], U8, align_bytes=64, name="fp_scales")
+        fc_codes = keep.tile([P, G, N], U32, align_bytes=64, name="fc_codes")
+        fc_scales = keep.tile([P, G, N], U8, align_bytes=64, name="fc_scales")
+        p_bf = keep.tile([P, G, N, 4], BF16, align_bytes=64, name="p_bf")
+        p_codes = keep.tile([P, G, N], U32, align_bytes=64, name="p_codes")
+        p_scales = keep.tile([P, G, N], U8, align_bytes=64, name="p_scales")
+        q_sb = keep.tile([P, 8, N], F32, align_bytes=64, name="q_sb")
+        R_codes = keep.tile([P, G, N], U32, align_bytes=64, name="R_codes")
+        R_scales = keep.tile([P, G, N], U8, align_bytes=64, name="R_scales")
+
+        nc.vector.memset(ws_sb[:].rearrange("p g n -> p (g n)").bitcast(I32), 0)
+
+        def load_a(g, c0, c1):
+            nc.sync.dma_start(out=a_sb[:, g, :, c0:c1], in_=a[512 * g : 512 * g + 512, c0:c1].rearrange("(p t) i -> p t i", t=4))
+
+        def load_gup(g, c0, c1):
+            nc.sync.dma_start(out=gup_sb[g][:, :, c0:c1], in_=gup[512 * g : 512 * g + 512, c0:c1].rearrange("(p t) i -> p t i", t=4))
+
+        load_a(0, 0, 512)
+        load_gup(0, 0, 512)
+        load_gup(0, 512, 1024)
+        load_gup(1, 0, 512)
+        load_gup(1, 512, 1024)
+        nc.sync.dma_start(out=w_sb[:].bitcast(I32), in_=w_words.rearrange("g p n -> p g n").bitcast(I32))
+        load_a(0, 512, 1024)
+        load_a(1, 0, 1024)
+        nc.gpsimd.dma_start(out=r_bf[:], in_=r.rearrange("(g p t) -> p g t", g=G, t=4))
+        nc.gpsimd.dma_start(out=c_bf[:], in_=c.rearrange("(g p t) -> p g t", g=G, t=4))
+        for Q in range(4):
+            nc.gpsimd.dma_start(
+                out=ws_sb[32 * Q : 32 * Q + 4, :, :].bitcast(I32),
+                in_=w_scales[:, 4 * Q : 4 * Q + 4, :].rearrange("g q n -> q g n").bitcast(I32),
+            )
+
+        make_identity(nc, ident[:])
+
+        fd = {}
+
+        def absolute(k):
+            g, c0 = k // 4, CH * (k % 4)
+            part = a_sb[:, g, :, c0 : c0 + CH].bitcast(I32)
+            nc.vector.tensor_scalar(out=part, in0=part, scalar1=0x7FFF7FFF, scalar2=None, op0=ALU.bitwise_and)
+
+        def cosine(k):
+            g, c0 = k // 4, CH * (k % 4)
+            nc.scalar.activation(out=cos_sb[:, k], in_=a_sb[:, g, :, c0 : c0 + CH], func=ACT.Sin, scale=-1.0, bias=math.pi / 2)
+
+        def times(k, factor, nm):
+            g = k // 4
+            t_f = stage.tile([P, CH, 4], BF16, align_bytes=64, name=nm)
+            fac = factor[:, 4 * g : 4 * g + 4].unsqueeze(1).unsqueeze(3).broadcast_to([P, CH // 4, 4, 4])
+            nc.vector.tensor_tensor(
+                out=t_f[:].rearrange("p (c i) t -> p c t i", i=4),
+                in0=cos_sb[:, k].rearrange("p t (c i) -> p c t i", i=4),
+                in1=fac, op=ALU.mult,
+            )
+            fd[nm, k] = t_f
+
+        def quant_f(k, nm, codes, scales):
+            g, c0 = k // 4, CH * (k % 4)
+            nc.vector.quantize_mx(
+                out=codes[:, g, c0 : c0 + CH].bitcast(E4M3), scales=scales[:, g, c0 : c0 + CH],
+                in_=fd[nm, k][:].rearrange("p i t -> p (i t)"),
+            )
+
+        gild = {}
+
+        def gup_tile(gk, ge):
+            t_g = stage.tile([P, 4, P, 4], BF16, align_bytes=64, name="t_g", tag="k4", bufs=4)
+            gild[gk, ge] = t_g
+
+        def gup_copy(gk, ge, t0, t1, eng):
+            src = gup_sb[gk][:, :, 512 * ge : 512 * ge + 512].rearrange("p j (m t) -> p t m j", t=4)
+            dst = gild[gk, ge]
+            if eng == 0:
+                nc.vector.tensor_copy(out=dst[:, t0:t1], in_=src[:, t0:t1])
+            else:
+                nc.scalar.copy(out=dst[:, t0:t1], in_=src[:, t0:t1])
+
+        def gup_quant(gk, ge):
+            nc.vector.quantize_mx(
+                out=g_codes[:, gk, 512 * ge : 512 * ge + 512].bitcast(E4M3), scales=g_scales[:, gk, 512 * ge : 512 * ge + 512],
+                in_=gild[gk, ge][:].rearrange("p t m j -> p (t m j)"),
+            )
+
+        pbank = {}
+
+        def stage1(dt, ge):
+            bank = psum.tile([P, 512], F32, name="bank")
+            for t in range(4):
+                for gk in range(G):
+                    e0 = 512 * ge + 128 * t
+                    nc.tensor.matmul_mx(
+                        out=bank[:, 128 * t : 128 * t + 128],
+                        lhsT=g_codes[:, gk, e0 : e0 + 128].bitcast(E4M3), lhsT_scale=g_scales[:, gk, e0 : e0 + 128],
+                        rhs=w_sb[:, gk, 256 * dt : 256 * dt + 256].bitcast(E2M1), rhs_scale=ws_sb[:, gk, 128 * dt : 128 * dt + 128],
+                        start=(gk == 0), stop=(gk == 1),
+                    )
+            pbank[dt, ge] = bank
+
+        def p_evac(dt, ge):
+            nc.scalar.copy(
+                out=p_bf[:, ge, 128 * dt : 128 * dt + 128, :],
+                in_=pbank[dt, ge][:].rearrange("p (t d) -> p d t", t=4),
+            )
+
+        def p_quant(ge, d0, d1):
+            nc.vector.quantize_mx(
+                out=p_codes[:, ge, d0:d1].bitcast(E4M3), scales=p_scales[:, ge, d0:d1],
+                in_=p_bf[:, ge, d0:d1, :].rearrange("p d t -> p (d t)"),
+            )
+
+        qbank = {}
+
+        def q_mm(dt, jh):
+            bank = psum.tile([P, 512], F32, name="bank")
+            for ge in range(G):
+                nc.tensor.matmul_mx(
+                    out=bank[:],
+                    lhsT=p_codes[:, ge, 128 * dt : 128 * dt + 128].bitcast(E4M3), lhsT_scale=p_scales[:, ge, 128 * dt : 128 * dt + 128],
+                    rhs=w_sb[:, ge, 1024 * jh : 1024 * jh + 1024].bitcast(E2M1), rhs_scale=ws_sb[:, ge, 512 * jh : 512 * jh + 512],
+                    start=(ge == 0), stop=(ge == 1),
+                )
+            qbank[dt, jh] = bank
+
+        def q_evac(dt, jh):
+            nc.scalar.activation(out=q_sb[:, dt, 512 * jh : 512 * jh + 512], in_=qbank[dt, jh][:], func=ACT.Copy, scale=1.0 / N)
+
+        mbank = {}
+
+        def m_mm(dt, jh):
+            bank = psum.tile([P, 512], F32, name="bank")
+            for g in range(G):
+                nc.tensor.matmul_mx(
+                    out=bank[:],
+                    lhsT=fc_codes[:, g, 128 * dt : 128 * dt + 128].bitcast(E4M3), lhsT_scale=fc_scales[:, g, 128 * dt : 128 * dt + 128],
+                    rhs=fp_codes[:, g, 512 * jh : 512 * jh + 512].bitcast(E4M3), rhs_scale=fp_scales[:, g, 512 * jh : 512 * jh + 512],
+                    start=(g == 0), stop=(g == 1),
+                )
+            mbank[dt, jh] = bank
+
+        Rd = {}
+        Rbd = {}
+
+        def product(dt):
+            t_R = stage.tile([P, N], F32, align_bytes=64, name="t_R", tag="k4", bufs=4)
+            for jh in range(2):
+                s = slice(512 * jh, 512 * jh + 512)
+                nc.vector.tensor_tensor(out=t_R[:, s], in0=mbank[dt, jh][:], in1=q_sb[:, dt, s], op=ALU.mult)
+            Rd[dt] = t_R
+
+        def store_R(dt):
+            nc.sync.dma_start(out=out_0[128 * dt : 128 * dt + 128, :], in_=Rd[dt][:])
+
+        def round_R(dt):
+            t_Rb = stage.tile([P, 2, 2, P, 2], BF16, align_bytes=64, name="t_Rb")
+            src = [Rd[dt][:, 512 * g : 512 * g + 512].rearrange("p (m u e) -> p u m e", u=2, e=2) for g in range(G)]
+            nc.gpsimd.tensor_scalar(out=t_Rb[:, 0], in0=src[0], scalar1=1.0, scalar2=1.0, op0=ALU.mult, op1=ALU.mult)
+            nc.scalar.copy(out=t_Rb[:, 1], in_=src[1])
+            Rbd[dt] = t_Rb
+
+        tbank = {}
+
+        def turn(dt):
+            bank = psum_t.tile([P, 2, 2, P], F32, name="tbank")
+            words = Rbd[dt][:].rearrange("p g u m e -> p (g u m e)").bitcast(F32)
+            for g in range(G):
+                for u in range(2):
+                    k = 2 * g + u
+                    nc.tensor.transpose(bank[:, g, u, :], words[:, 128 * k : 128 * k + 128], ident[:])
+            tbank[dt] = bank
+
+        y_tile = {}
+
+        def y_open(h):
+            t_y = keep.tile([P, G, 512, 4], BF16, align_bytes=64, name="raw", bufs=2)
+            y_tile[h] = t_y
+
+        def y_evac(dt):
+            d0 = 128 * (dt % 4)
+            dst = y_tile[dt // 4][:].rearrange("p g d t -> p (g d t)").bitcast(F32).rearrange("p (g d u) -> p g d u", g=G, u=2)
+            nc.scalar.copy(out=dst[:, :, d0 : d0 + 128, :], in_=tbank[dt][:].rearrange("p g u d -> p g d u"))
+
+        def y_quant(h, d0, d1):
+            for g in range(G):
+                nc.vector.quantize_mx(
+                    out=R_codes[:, g, 512 * h + d0 : 512 * h + d1].bitcast(E4M3), scales=R_scales[:, g, 512 * h + d0 : 512 * h + d1],
+                    in_=y_tile[h][:, g, d0:d1, :].rearrange("p d t -> p (d t)"),
+                )
+
+        def y_store(m0, m1):
+            nc.sync.dma_start(
+                out=out_1[:, :, m0:m1, :].rearrange("g p m t -> p g (m t)").bitcast(I32),
+                in_=R_codes[:, :, m0:m1].bitcast(I32),
+            )
+            for Q in range(4):
+                nc.sync.dma_start(
+                    out=out_2[:, 4 * Q : 4 * Q + 4, m0:m1].rearrange("g q m -> q g m").bitcast(I32),
+                    in_=R_scales[32 * Q : 32 * Q + 4, :, m0:m1].bitcast(I32),
+                )
+
+        absolute(0)
+        absolute(1)
+        cosine(0)
+        chunks = [(0, 0), (0, 1), (1, 0), (1, 1)]
+        for k in range(4):
+            gup_tile(*chunks[k])
+            gup_copy(*chunks[k], 0, 2, 0)
+            gup_copy(*chunks[k], 2, 4, 1)
+            if k == 1:
+                nc.vector.tensor_copy(out=r_f[:], in_=r_bf[:].rearrange("p g t -> p (g t)"))
+                nc.vector.tensor_tensor(out=cr_f[:], in0=c_bf[:].rearrange("p g t -> p (g t)"), in1=r_bf[:].rearrange("p g t -> p (g t)"), op=ALU.mult)
+            if k > 0:
+                gup_quant(*chunks[k - 1])
+        times(0, r_f, "t_fp")
+        gup_quant(1, 1)
+        cosine(1)
+
+        def s1(dt):
+            stage1(dt, 0)
+            stage1(dt, 1)
+
+        def pq(i):
+            p_quant(0, 256 * i, 256 * i + 256)
+            p_quant(1, 256 * i, 256 * i + 256)
+
+        def q2(dt):
+            q_mm(dt, 0)
+            q_mm(dt, 1)
+
+        pend = []
+
+        def unit(k, nm):
+            if nm == "t_fp":
+                times(k, r_f, nm)
+            else:
+                times(k, cr_f, nm)
+            flush(0)
+            pend.append((k, nm))
+
+        def flush(n):
+            while len(pend) > n:
+                k, nm = pend.pop(0)
+                if nm == "t_fp":
+                    quant_f(k, nm, fp_codes, fp_scales)
+                else:
+                    quant_f(k, nm, fc_codes, fc_scales)
+
+        evq = [("p", dt, h) for dt in range(4) for h in range(2)]
+        for i in range(3):
+            evq += [("q", dt, h) for dt in (2 * i, 2 * i + 1) for h in range(2)]
+            if i < 2:
+                evq += [("p", dt, h) for dt in (4 + 2 * i, 5 + 2 * i) for h in range(2)]
+        evq += [("q", dt, h) for dt in (6, 7) for h in range(2)]
+
+        def ev(n):
+            for unused in range(n):
+                if evq:
+                    what, dt, h = evq.pop(0)
+                    if what == "p":
+                        p_evac(dt, h)
+                    else:
+                        q_evac(dt, h)
+
+        pend.append((0, "t_fp"))
+        for dt in range(4):
+            s1(dt)
+        deferred = [2,6,3,7]
+        nev = [3,3,3,3,3,3,3,3]
+        absolute(2)
+        absolute(3)
+        for k in range(NCH):
+            if k > 0:
+                unit(k, "t_fp")
+            if 1 < k + 3 < NCH and k > 0:
+                absolute(k + 3)
+            if k not in deferred:
+                unit(k, "t_fc")
+            if k + 2 < NCH:
+                cosine(k + 2)
+            if k == 2:
+                pq(0)
+                q2(0)
+                q2(1)
+                s1(4)
+                s1(5)
+            if k == 3:
+                pq(1)
+                q2(2)
+                q2(3)
+                s1(6)
+                s1(7)
+            if k == 6:
+                pq(2)
+                q2(4)
+                q2(5)
+            ev(nev[k])
+        pq(3)
+        flush(0)
+
+        y_open(0)
+        y_open(1)
+
+        def mp(dt):
+            m_mm(dt, 0)
+            m_mm(dt, 1)
+
+        def out(dt):
+            product(dt)
+            store_R(dt)
+            round_R(dt)
+
+        def tr(dt):
+            turn(dt)
+            y_evac(dt)
+
+        late = [(2, "t_fc"), (6, "t_fc"), (3, "t_fc"), (7, "t_fc")]
+        mp(0)
+        mp(1)
+        q2(6)
+        q2(7)
+        product(0)
+        store_R(0)
+        if late:
+            unit(*late.pop(0))
+        product(1)
+        store_R(1)
+        if late:
+            unit(*late.pop(0))
+        flush(0)
+        ev(2)
+        round_R(0)
+        ev(2)
+        round_R(1)
+        ev(8)
+        mp(2)
+        tr(0)
+        tr(1)
+        mp(3)
+        out(2)
+        if late:
+            unit(*late.pop(0))
+        out(3)
+        if late:
+            unit(*late.pop(0))
+        flush(0)
+        mp(4)
+        tr(2)
+        tr(3)
+        mp(5)
+        out(4)
+        out(5)
+        y_quant(0, 0, 512)
+        y_store(0, 512)
+        mp(6)
+        tr(4)
+        tr(5)
+        mp(7)
+        out(6)
+        out(7)
+        y_quant(1, 0, 256)
+        tr(6)
+        tr(7)
+        y_quant(1, 256, 512)
+        y_store(512, 1024)

@@ -21,6 +21,12 @@ G = 2
 P = 128
 CH = 256
 NCH = 8
+PSUM_FACTORS = False
+ON_G = []
+ON_S = []
+GS = 2
+YG = [[0,4],[4,6],[6,8]]
+RND = ["G","S"]
 
 
 def tile_kfrasinecurvaturepullback_x2_kernel(tc, w_words, w_scales, gup, a, r, c, out_0, out_1, out_2):
@@ -30,110 +36,176 @@ def tile_kfrasinecurvaturepullback_x2_kernel(tc, w_words, w_scales, gup, a, r, c
         stage = ctx.enter_context(tc.tile_pool(name="stage", bufs=3))
         psum = ctx.enter_context(tc.psum_pool(name="psum", bufs=6))
         psum_t = ctx.enter_context(tc.psum_pool(name="psum_t", bufs=2))
+        psum_f = ctx.enter_context(tc.psum_pool(name="psum_f", bufs=1))
         ctx.enter_context(tc.manual_schedule())
 
-        a_sb = keep.tile([P, G, 4, N], BF16, align_bytes=64, name="a_sb")
-        gup_sb = []
-        for g in range(G):
-            gup_half = keep.tile([P, 4, N], BF16, align_bytes=64, name="raw", bufs=2)
-            gup_sb.append(gup_half)
-        cos_sb = keep.tile([P, NCH, 4, CH], F32, align_bytes=64, name="cos_sb")
-        w_sb = keep.tile([P, G, 2 * N], U8, align_bytes=64, name="w_sb")
-        ws_sb = keep.tile([P, G, N], U8, align_bytes=64, name="ws_sb")
-        r_bf = keep.tile([P, G, 4], BF16, align_bytes=64, name="r_bf")
-        c_bf = keep.tile([P, G, 4], BF16, align_bytes=64, name="c_bf")
-        r_f = keep.tile([P, G * 4], F32, align_bytes=64, name="r_f")
-        cr_f = keep.tile([P, G * 4], F32, align_bytes=64, name="cr_f")
-        ident = keep.tile([P, P], F32, align_bytes=64, name="ident")
-        g_codes = keep.tile([P, G, N], U32, align_bytes=64, name="g_codes")
-        g_scales = keep.tile([P, G, N], U8, align_bytes=64, name="g_scales")
-        fp_codes = keep.tile([P, G, N], U32, align_bytes=64, name="fp_codes")
-        fp_scales = keep.tile([P, G, N], U8, align_bytes=64, name="fp_scales")
-        fc_codes = keep.tile([P, G, N], U32, align_bytes=64, name="fc_codes")
-        fc_scales = keep.tile([P, G, N], U8, align_bytes=64, name="fc_scales")
-        p_bf = keep.tile([P, G, N, 4], BF16, align_bytes=64, name="p_bf")
-        p_codes = keep.tile([P, G, N], U32, align_bytes=64, name="p_codes")
-        p_scales = keep.tile([P, G, N], U8, align_bytes=64, name="p_scales")
-        q_sb = keep.tile([P, 8, N], F32, align_bytes=64, name="q_sb")
-        R_codes = keep.tile([P, G, N], U32, align_bytes=64, name="R_codes")
-        R_scales = keep.tile([P, G, N], U8, align_bytes=64, name="R_scales")
+        def made(pool, shape, dtype, name, tag=None, bufs=1):
+            return pool.tile(shape, dtype, align_bytes=64, name=name, tag=tag or name, bufs=bufs)
+
+        a_cols = [[0,0,256],[0,256,512],[0,512,1024],[1,0,1024]]
+        a_sb = []
+        for i, (g, c0, c1) in enumerate(a_cols):
+            a_sb.append(made(keep, [P, 4, c1 - c0], BF16, "a%d" % i))
+        g_raw = {}
+        for gk in range(G):
+            for ge in range(G):
+                g_raw[gk, ge] = made(keep, [P, 4, 512], BF16, "g_raw%d%d" % (gk, ge), "big", 4)
+        w_sb = made(keep, [P, G, 2 * N], U8, "w_sb")
+        ws_sb = made(keep, [P, G, N], U8, "ws_sb")
+        r_bf = made(keep, [P, G * 4], BF16, "r_bf")
+        c_bf = made(keep, [P, G * 4], BF16, "c_bf")
+        ident = made(keep, [P, P], F32, "ident")
+        fac = made(keep, [P, P], F32, "fac")
+        g_codes = made(keep, [P, G, N], U32, "g_codes")
+        g_scales = made(keep, [P, G, N], U8, "g_scales")
+        fp_codes = made(keep, [P, G, N], U32, "fp_codes")
+        fp_scales = made(keep, [P, G, N], U8, "fp_scales")
+        fc_codes = made(keep, [P, G, N], U32, "fc_codes")
+        fc_scales = made(keep, [P, G, N], U8, "fc_scales")
+        cos_sb = made(keep, [P, NCH, 4, CH], F32, "cos_sb")
+        p_bf = made(keep, [P, G, N, 4], BF16, "p_bf")
+        p_codes = made(keep, [P, G, N], U32, "p_codes")
+        p_scales = made(keep, [P, G, N], U8, "p_scales")
+        q_sb = made(keep, [P, 8, N], F32, "q_sb")
+        if PSUM_FACTORS:
+            fac_t = made(keep, [P, P], F32, "fac_t")
+            fac_ps = psum_f.tile([P, 2, P], F32, name="fac_ps")
 
         nc.vector.memset(ws_sb[:].rearrange("p g n -> p (g n)").bitcast(I32), 0)
+        if PSUM_FACTORS:
+            nc.gpsimd.memset(fac[:], 0.0)
 
-        def load_a(g, c0, c1):
-            nc.sync.dma_start(out=a_sb[:, g, :, c0:c1], in_=a[512 * g : 512 * g + 512, c0:c1].rearrange("(p t) i -> p t i", t=4))
+        def load_a(i):
+            g, c0, c1 = a_cols[i]
+            nc.sync.dma_start(out=a_sb[i][:], in_=a[512 * g : 512 * g + 512, c0:c1].rearrange("(p t) i -> p t i", t=4))
 
-        def load_gup(g, c0, c1):
-            nc.sync.dma_start(out=gup_sb[g][:, :, c0:c1], in_=gup[512 * g : 512 * g + 512, c0:c1].rearrange("(p t) i -> p t i", t=4))
-
-        load_a(0, 0, 512)
-        load_gup(0, 0, 512)
-        load_gup(0, 512, 1024)
-        load_gup(1, 0, 512)
-        load_gup(1, 512, 1024)
-        nc.sync.dma_start(out=w_sb[:].bitcast(I32), in_=w_words.rearrange("g p n -> p g n").bitcast(I32))
-        load_a(0, 512, 1024)
-        load_a(1, 0, 1024)
-        nc.gpsimd.dma_start(out=r_bf[:], in_=r.rearrange("(g p t) -> p g t", g=G, t=4))
-        nc.gpsimd.dma_start(out=c_bf[:], in_=c.rearrange("(g p t) -> p g t", g=G, t=4))
-        for Q in range(4):
-            nc.gpsimd.dma_start(
-                out=ws_sb[32 * Q : 32 * Q + 4, :, :].bitcast(I32),
-                in_=w_scales[:, 4 * Q : 4 * Q + 4, :].rearrange("g q n -> q g n").bitcast(I32),
+        def load_g(gk, ge):
+            nc.sync.dma_start(
+                out=g_raw[gk, ge][:], in_=gup[512 * gk : 512 * gk + 512, 512 * ge : 512 * ge + 512].rearrange("(p t) e -> p t e", t=4)
             )
 
-        make_identity(nc, ident[:])
+        def load_w():
+            nc.sync.dma_start(out=w_sb[:].bitcast(I32), in_=w_words.rearrange("g p n -> p g n").bitcast(I32))
 
-        fd = {}
+        def load_ws(eng):
+            for Q in range(4):
+                eng.dma_start(
+                    out=ws_sb[32 * Q : 32 * Q + 4, :, :].bitcast(I32),
+                    in_=w_scales[:, 4 * Q : 4 * Q + 4, :].rearrange("g q n -> q g n").bitcast(I32),
+                )
+
+        nc.gpsimd.dma_start(out=r_bf[:].rearrange("p (g t) -> p g t", g=G), in_=r.rearrange("(g p t) -> p g t", g=G, t=4))
+        nc.gpsimd.dma_start(out=c_bf[:].rearrange("p (g t) -> p g t", g=G), in_=c.rearrange("(g p t) -> p g t", g=G, t=4))
+        make_identity(nc, ident[:])
+        load_a(0)
+        load_g(0, 0)
+        load_ws(nc.sync)
+        load_g(1, 0)
+        load_w()
+        load_a(1)
+        load_g(0, 1)
+        load_g(1, 1)
+        load_a(2)
+        load_a(3)
+
+        ops = {}
+
+        def op(name, needs):
+            def put(fn):
+                ops[name] = (fn, needs)
+            return put
+
+        t_abs = {}
+        t_f = {}
+        t_g = {}
+        banks = {}
+        t_R = {}
+        t_Rb = {}
+        t_y = {}
+        y_codes = {}
+        y_scales = {}
 
         def absolute(k):
             g, c0 = k // 4, CH * (k % 4)
-            part = a_sb[:, g, :, c0 : c0 + CH].bitcast(I32)
-            nc.vector.tensor_scalar(out=part, in0=part, scalar1=0x7FFF7FFF, scalar2=None, op0=ALU.bitwise_and)
+            for i, (ga, a0, a1) in enumerate(a_cols):
+                if ga == g and a0 <= c0 < a1:
+                    src = a_sb[i][:, :, c0 - a0 : c0 - a0 + CH]
+            t_abs[k] = made(stage, [P, 4, CH], BF16, "t_abs", None, 8)
+            nc.vector.tensor_scalar(
+                out=t_abs[k][:].bitcast(I32), in0=src.bitcast(I32), scalar1=0x7FFF7FFF, scalar2=None, op0=ALU.bitwise_and
+            )
 
         def cosine(k):
-            g, c0 = k // 4, CH * (k % 4)
-            nc.scalar.activation(out=cos_sb[:, k], in_=a_sb[:, g, :, c0 : c0 + CH], func=ACT.Sin, scale=-1.0, bias=math.pi / 2)
+            nc.scalar.activation(out=cos_sb[:, k], in_=t_abs[k][:], func=ACT.Sin, scale=-1.0, bias=math.pi / 2)
 
-        def times(k, factor, nm):
-            g = k // 4
-            t_f = stage.tile([P, CH, 4], BF16, align_bytes=64, name=nm)
-            fac = factor[:, 4 * g : 4 * g + 4].unsqueeze(1).unsqueeze(3).broadcast_to([P, CH // 4, 4, 4])
-            nc.vector.tensor_tensor(
-                out=t_f[:].rearrange("p (c i) t -> p c t i", i=4),
-                in0=cos_sb[:, k].rearrange("p t (c i) -> p c t i", i=4),
-                in1=fac, op=ALU.mult,
-            )
-            fd[nm, k] = t_f
+        def factors():
+            nc.vector.tensor_copy(out=fac[:, 0:8], in_=r_bf[:])
+            nc.vector.tensor_tensor(out=fac[:, 8:16], in0=c_bf[:], in1=r_bf[:], op=ALU.mult)
 
-        def quant_f(k, nm, codes, scales):
+        def factor_turn(i):
+            nc.tensor.transpose(fac_ps[:, i, :], (fac, fac_t)[i][:], ident[:])
+
+        def factor_copy():
+            nc.vector.tensor_copy(out=fac_t[:], in_=fac_ps[:, 0, :])
+
+        def factor(nm, k, where):
+            c0 = (8 if nm == "fc" else 0) + 4 * (k // 4)
+            return where[:, c0 : c0 + 4]
+
+        def times(nm, k):
+            tile = made(stage, [P, CH, 4], BF16, "t_f", None, 6)
+            if (nm, k) in ON_G:
+                for h in range(GS):
+                    s = slice(CH // GS * h, CH // GS * h + CH // GS)
+                    nc.gpsimd.tensor_tensor(
+                        out=tile[:, s, :], in0=cos_sb[:, k, :, s].rearrange("p t i -> p i t"),
+                        in1=factor(nm, k, fac).unsqueeze(1).broadcast_to([P, CH // GS, 4]), op=ALU.mult,
+                    )
+            else:
+                where = fac_ps[:, 1, :] if PSUM_FACTORS else fac
+                nc.vector.tensor_tensor(
+                    out=tile[:].rearrange("p (c i) t -> p c t i", i=4),
+                    in0=cos_sb[:, k].rearrange("p t (c i) -> p c t i", i=4),
+                    in1=factor(nm, k, where).unsqueeze(1).unsqueeze(3).broadcast_to([P, CH // 4, 4, 4]), op=ALU.mult,
+                )
+            t_f[nm, k] = tile
+
+        def rows(nm, k):
+            tile = made(stage, [P, 4, CH], BF16, "t_rows", None, 2)
+            for t in range(4):
+                c0 = (8 if nm == "fc" else 0) + 4 * (k // 4) + t
+                nc.vector.tensor_scalar(out=tile[:, t, :], in0=cos_sb[:, k, t, :], scalar1=fac[:, c0 : c0 + 1], scalar2=None, op0=ALU.mult)
+            t_f[nm + "m", k] = tile
+
+        def weave_rows(nm, k):
+            tile = made(stage, [P, CH, 4], BF16, "t_f", None, 6)
+            nc.scalar.copy(out=tile[:].rearrange("p (c i) t -> p c t i", i=4), in_=t_f[nm + "m", k][:].rearrange("p t (c i) -> p c t i", i=4))
+            t_f[nm, k] = tile
+
+        def quant_f(nm, k):
             g, c0 = k // 4, CH * (k % 4)
+            codes, scales = (fp_codes, fp_scales) if nm == "fp" else (fc_codes, fc_scales)
             nc.vector.quantize_mx(
                 out=codes[:, g, c0 : c0 + CH].bitcast(E4M3), scales=scales[:, g, c0 : c0 + CH],
-                in_=fd[nm, k][:].rearrange("p i t -> p (i t)"),
+                in_=t_f[nm, k][:].rearrange("p i t -> p (i t)"),
             )
 
-        gild = {}
-
-        def gup_tile(gk, ge):
-            t_g = stage.tile([P, 4, P, 4], BF16, align_bytes=64, name="t_g", tag="k4", bufs=4)
-            gild[gk, ge] = t_g
-
-        def gup_copy(gk, ge, t0, t1, eng):
-            src = gup_sb[gk][:, :, 512 * ge : 512 * ge + 512].rearrange("p j (m t) -> p t m j", t=4)
-            dst = gild[gk, ge]
-            if eng == 0:
-                nc.vector.tensor_copy(out=dst[:, t0:t1], in_=src[:, t0:t1])
-            else:
-                nc.scalar.copy(out=dst[:, t0:t1], in_=src[:, t0:t1])
+        def gup_copy(gk, ge, eng):
+            if (gk, ge) not in t_g:
+                t_g[gk, ge] = made(stage, [P, 4, P, 4], BF16, "t_g", "k4", 4)
+            src = g_raw[gk, ge][:].rearrange("p j (m t) -> p t m j", t=4)
+            dst = t_g[gk, ge]
+            v = {(0, 0): 2, (1, 0): 2, (0, 1): 2, (1, 1): 2}[gk, ge]
+            if eng == "V" and v > 0:
+                nc.vector.tensor_copy(out=dst[:, 0:v], in_=src[:, 0:v])
+            if eng == "S" and v < 4:
+                nc.scalar.copy(out=dst[:, v:4], in_=src[:, v:4])
 
         def gup_quant(gk, ge):
             nc.vector.quantize_mx(
                 out=g_codes[:, gk, 512 * ge : 512 * ge + 512].bitcast(E4M3), scales=g_scales[:, gk, 512 * ge : 512 * ge + 512],
-                in_=gild[gk, ge][:].rearrange("p t m j -> p (t m j)"),
+                in_=t_g[gk, ge][:].rearrange("p t m j -> p (t m j)"),
             )
-
-        pbank = {}
 
         def stage1(dt, ge):
             bank = psum.tile([P, 512], F32, name="bank")
@@ -146,21 +218,24 @@ def tile_kfrasinecurvaturepullback_x2_kernel(tc, w_words, w_scales, gup, a, r, c
                         rhs=w_sb[:, gk, 256 * dt : 256 * dt + 256].bitcast(E2M1), rhs_scale=ws_sb[:, gk, 128 * dt : 128 * dt + 128],
                         start=(gk == 0), stop=(gk == 1),
                     )
-            pbank[dt, ge] = bank
+            banks["p", dt, ge] = bank
 
         def p_evac(dt, ge):
-            nc.scalar.copy(
-                out=p_bf[:, ge, 128 * dt : 128 * dt + 128, :],
-                in_=pbank[dt, ge][:].rearrange("p (t d) -> p d t", t=4),
-            )
+            dst = p_bf[:, ge, 128 * dt : 128 * dt + 128, :]
+            src = banks["p", dt, ge][:].rearrange("p (t d) -> p d t", t=4)
+            nc.scalar.copy(out=dst, in_=src)
 
-        def p_quant(ge, d0, d1):
+        def p_evac_v(dt, ge):
+            dst = p_bf[:, ge, 128 * dt : 128 * dt + 128, :]
+            src = banks["p", dt, ge][:].rearrange("p (t d) -> p d t", t=4)
+            nc.vector.tensor_copy(out=dst, in_=src)
+
+        def p_quant(d0, d1, ge):
+            s = slice(128 * d0, 128 * d1)
             nc.vector.quantize_mx(
-                out=p_codes[:, ge, d0:d1].bitcast(E4M3), scales=p_scales[:, ge, d0:d1],
-                in_=p_bf[:, ge, d0:d1, :].rearrange("p d t -> p (d t)"),
+                out=p_codes[:, ge, s].bitcast(E4M3), scales=p_scales[:, ge, s],
+                in_=p_bf[:, ge, s, :].rearrange("p d t -> p (d t)"),
             )
-
-        qbank = {}
 
         def q_mm(dt, jh):
             bank = psum.tile([P, 512], F32, name="bank")
@@ -171,12 +246,10 @@ def tile_kfrasinecurvaturepullback_x2_kernel(tc, w_words, w_scales, gup, a, r, c
                     rhs=w_sb[:, ge, 1024 * jh : 1024 * jh + 1024].bitcast(E2M1), rhs_scale=ws_sb[:, ge, 512 * jh : 512 * jh + 512],
                     start=(ge == 0), stop=(ge == 1),
                 )
-            qbank[dt, jh] = bank
+            banks["q", dt, jh] = bank
 
         def q_evac(dt, jh):
-            nc.scalar.activation(out=q_sb[:, dt, 512 * jh : 512 * jh + 512], in_=qbank[dt, jh][:], func=ACT.Copy, scale=1.0 / N)
-
-        mbank = {}
+            nc.scalar.activation(out=q_sb[:, dt, 512 * jh : 512 * jh + 512], in_=banks["q", dt, jh][:], func=ACT.Copy, scale=1.0 / N)
 
         def m_mm(dt, jh):
             bank = psum.tile([P, 512], F32, name="bank")
@@ -187,229 +260,148 @@ def tile_kfrasinecurvaturepullback_x2_kernel(tc, w_words, w_scales, gup, a, r, c
                     rhs=fp_codes[:, g, 512 * jh : 512 * jh + 512].bitcast(E4M3), rhs_scale=fp_scales[:, g, 512 * jh : 512 * jh + 512],
                     start=(g == 0), stop=(g == 1),
                 )
-            mbank[dt, jh] = bank
+            banks["m", dt, jh] = bank
 
-        Rd = {}
-        Rbd = {}
-
-        def product(dt):
-            t_R = stage.tile([P, N], F32, align_bytes=64, name="t_R", tag="k4", bufs=4)
-            for jh in range(2):
-                s = slice(512 * jh, 512 * jh + 512)
-                nc.vector.tensor_tensor(out=t_R[:, s], in0=mbank[dt, jh][:], in1=q_sb[:, dt, s], op=ALU.mult)
-            Rd[dt] = t_R
+        def product(dt, jh):
+            if dt not in t_R:
+                t_R[dt] = made(stage, [P, N], F32, "t_R", "k4", 4)
+            s = slice(512 * jh, 512 * jh + 512)
+            nc.vector.tensor_tensor(out=t_R[dt][:, s], in0=banks["m", dt, jh][:], in1=q_sb[:, dt, s], op=ALU.mult)
 
         def store_R(dt):
-            nc.sync.dma_start(out=out_0[128 * dt : 128 * dt + 128, :], in_=Rd[dt][:])
+            nc.sync.dma_start(out=out_0[128 * dt : 128 * dt + 128, :], in_=t_R[dt][:])
 
-        def round_R(dt):
-            t_Rb = stage.tile([P, 2, 2, P, 2], BF16, align_bytes=64, name="t_Rb")
-            src = [Rd[dt][:, 512 * g : 512 * g + 512].rearrange("p (m u e) -> p u m e", u=2, e=2) for g in range(G)]
-            nc.gpsimd.tensor_scalar(out=t_Rb[:, 0], in0=src[0], scalar1=1.0, scalar2=1.0, op0=ALU.mult, op1=ALU.mult)
-            nc.scalar.copy(out=t_Rb[:, 1], in_=src[1])
-            Rbd[dt] = t_Rb
-
-        tbank = {}
+        def round_R(dt, h):
+            if dt not in t_Rb:
+                t_Rb[dt] = made(stage, [P, 2, 2, P, 2], BF16, "t_Rb", None, 3)
+            src = t_R[dt][:, 512 * h : 512 * h + 512].rearrange("p (m u e) -> p u m e", u=2, e=2)
+            dst = t_Rb[dt][:, h]
+            if RND[h] == "G":
+                nc.gpsimd.tensor_scalar(out=dst, in0=src, scalar1=1.0, scalar2=1.0, op0=ALU.mult, op1=ALU.mult)
+            elif RND[h] == "V":
+                nc.vector.tensor_copy(out=dst, in_=src)
+            else:
+                nc.scalar.copy(out=dst, in_=src)
 
         def turn(dt):
             bank = psum_t.tile([P, 2, 2, P], F32, name="tbank")
-            words = Rbd[dt][:].rearrange("p g u m e -> p (g u m e)").bitcast(F32)
+            words = t_Rb[dt][:].rearrange("p g u m e -> p (g u m e)").bitcast(F32)
             for g in range(G):
                 for u in range(2):
                     k = 2 * g + u
                     nc.tensor.transpose(bank[:, g, u, :], words[:, 128 * k : 128 * k + 128], ident[:])
-            tbank[dt] = bank
+            banks["t", dt] = bank
 
-        y_tile = {}
-
-        def y_open(h):
-            t_y = keep.tile([P, G, 512, 4], BF16, align_bytes=64, name="raw", bufs=2)
-            y_tile[h] = t_y
+        def group(dt):
+            for i, (d0, d1) in enumerate(YG):
+                if d0 <= dt < d1:
+                    return i, d0, d1
 
         def y_evac(dt):
-            d0 = 128 * (dt % 4)
-            dst = y_tile[dt // 4][:].rearrange("p g d t -> p (g d t)").bitcast(F32).rearrange("p (g d u) -> p g d u", g=G, u=2)
-            nc.scalar.copy(out=dst[:, :, d0 : d0 + 128, :], in_=tbank[dt][:].rearrange("p g u d -> p g d u"))
+            i, d0, d1 = group(dt)
+            w = 128 * (d1 - d0)
+            if i not in t_y:
+                t_y[i] = made(keep, [P, G, w, 4], BF16, "t_y%d" % i, "big" if w == 256 else None, 4 if w == 256 else 1)
+            dst = t_y[i][:].rearrange("p g d t -> p (g d t)").bitcast(F32).rearrange("p (g d u) -> p g d u", g=G, u=2)
+            s = slice(128 * (dt - d0), 128 * (dt - d0) + 128)
+            nc.scalar.copy(out=dst[:, :, s, :], in_=banks["t", dt][:].rearrange("p g u d -> p g d u"))
 
-        def y_quant(h, d0, d1):
-            for g in range(G):
-                nc.vector.quantize_mx(
-                    out=R_codes[:, g, 512 * h + d0 : 512 * h + d1].bitcast(E4M3), scales=R_scales[:, g, 512 * h + d0 : 512 * h + d1],
-                    in_=y_tile[h][:, g, d0:d1, :].rearrange("p d t -> p (d t)"),
-                )
-
-        def y_store(m0, m1):
-            nc.sync.dma_start(
-                out=out_1[:, :, m0:m1, :].rearrange("g p m t -> p g (m t)").bitcast(I32),
-                in_=R_codes[:, :, m0:m1].bitcast(I32),
+        def y_quant(i, g):
+            d0, d1 = YG[i]
+            w = 128 * (d1 - d0)
+            if i not in y_codes:
+                y_codes[i] = made(keep, [P, G, w], U32, "y_codes%d" % i)
+                y_scales[i] = made(keep, [P, G, w], U8, "y_scales%d" % i)
+            nc.vector.quantize_mx(
+                out=y_codes[i][:, g, :].bitcast(E4M3), scales=y_scales[i][:, g, :],
+                in_=t_y[i][:, g, :, :].rearrange("p d t -> p (d t)"),
             )
+
+        def y_store(i):
+            m0, m1 = 128 * YG[i][0], 128 * YG[i][1]
+            nc.sync.dma_start(
+                out=out_1[:, :, m0:m1, :].rearrange("g p m t -> p g (m t)").bitcast(I32), in_=y_codes[i][:].bitcast(I32)
+            )
+
+        def s_store(i):
+            m0, m1 = 128 * YG[i][0], 128 * YG[i][1]
             for Q in range(4):
                 nc.sync.dma_start(
                     out=out_2[:, 4 * Q : 4 * Q + 4, m0:m1].rearrange("g q m -> q g m").bitcast(I32),
-                    in_=R_scales[32 * Q : 32 * Q + 4, :, m0:m1].bitcast(I32),
+                    in_=y_scales[i][32 * Q : 32 * Q + 4, :, :].bitcast(I32),
                 )
 
-        absolute(0)
-        absolute(1)
-        cosine(0)
-        chunks = [(0, 0), (0, 1), (1, 0), (1, 1)]
-        for k in range(4):
-            gup_tile(*chunks[k])
-            gup_copy(*chunks[k], 0, 2, 0)
-            gup_copy(*chunks[k], 2, 4, 1)
-            if k == 1:
-                nc.vector.tensor_copy(out=r_f[:], in_=r_bf[:].rearrange("p g t -> p (g t)"))
-                nc.vector.tensor_tensor(out=cr_f[:], in0=c_bf[:].rearrange("p g t -> p (g t)"), in1=r_bf[:].rearrange("p g t -> p (g t)"), op=ALU.mult)
-            if k > 0:
-                gup_quant(*chunks[k - 1])
-        times(0, r_f, "t_fp")
-        gup_quant(1, 1)
-        cosine(1)
+        VEC = [("abs", 0), ("gv", 0, 0), ("fac",), ("fc", 0), ("gv", 1, 0), ("fp", 0), ("abs", 1), ("gq", 1, 0), ("gv", 0, 1), ("qfp", 0), ("gq", 0, 0), ("gv", 1, 1), ("gq", 0, 1), ("abs", 2), ("abs", 3), ("gq", 1, 1), ("fp", 1), ("fp", 2), ("abs", 4), ("abs", 5), ("fc", 1), ("abs", 6), ("fp", 3), ("pq", 0, 2, 0), ("abs", 7), ("pq", 0, 2, 1), ("qfc", 0), ("fc", 4), ("qfp", 1), ("fp", 4), ("pq", 2, 4, 1), ("qfc", 1), ("qfp", 2), ("qfp", 3), ("fp", 5), ("pq", 2, 4, 0), ("fc", 5), ("qfp", 4), ("qfp", 5), ("qfc", 4), ("fp", 6), ("qfc", 5), ("fp", 7), ("qfp", 6), ("pq", 4, 6, 1), ("qfp", 7), ("fc", 2), ("pq", 4, 6, 0), ("pr", 0, 0), ("qfc", 2), ("pr", 0, 1), ("pr", 1, 0), ("fc", 6), ("fc", 3), ("qfc", 6), ("pr", 1, 1), ("pr", 2, 0), ("pr", 2, 1), ("pr", 3, 0), ("pr", 3, 1), ("pr", 4, 0), ("pq", 6, 8, 1), ("pq", 6, 8, 0), ("pr", 4, 1), ("pr", 5, 0), ("fc", 7), ("qfc", 3), ("qfc", 7), ("pr", 5, 1), ("yq", 0, 1), ("yq", 0, 0), ("pr", 6, 0), ("pr", 6, 1), ("pr", 7, 0), ("pr", 7, 1), ("yq", 1, 1), ("yq", 1, 0), ("yq", 2, 0), ("yq", 2, 1)]
+        SCA = [("cos", 0), ("gs", 1, 0), ("gs", 0, 0), ("cos", 1), ("gs", 0, 1), ("gs", 1, 1), ("pe", 0, 0), ("cos", 2), ("cos", 3), ("pe", 0, 1), ("pe", 1, 0), ("pe", 1, 1), ("cos", 4), ("pe", 2, 1), ("pe", 2, 0), ("pe", 3, 1), ("cos", 5), ("cos", 6), ("pe", 3, 0), ("pe", 4, 0), ("pe", 4, 1), ("qe", 0, 0), ("pe", 5, 0), ("qe", 0, 1), ("qe", 1, 0), ("cos", 7), ("pe", 5, 1), ("qe", 1, 1), ("qe", 2, 0), ("qe", 2, 1), ("pe", 6, 0), ("qe", 3, 0), ("pe", 6, 1), ("pe", 7, 1), ("qe", 3, 1), ("qe", 4, 0), ("pe", 7, 0), ("rd", 0, 1), ("y", 0), ("qe", 4, 1), ("qe", 5, 0), ("rd", 1, 1), ("rd", 2, 1), ("rd", 3, 1), ("y", 1), ("qe", 5, 1), ("y", 2), ("rd", 4, 1), ("qe", 6, 0), ("qe", 6, 1), ("y", 3), ("y", 4), ("qe", 7, 0), ("qe", 7, 1), ("rd", 5, 1), ("rd", 6, 1), ("y", 5), ("rd", 7, 1), ("y", 6), ("y", 7)]
+        TEN = [("s1", 0, 0), ("s1", 0, 1), ("s1", 1, 0), ("s1", 1, 1), ("s1", 2, 0), ("s1", 2, 1), ("s1", 3, 1), ("s1", 4, 1), ("s1", 3, 0), ("s1", 4, 0), ("q", 0, 0), ("s1", 5, 1), ("q", 0, 1), ("q", 1, 0), ("s1", 5, 0), ("s1", 6, 0), ("q", 1, 1), ("s1", 6, 1), ("q", 2, 0), ("q", 2, 1), ("q", 3, 0), ("m", 0, 0), ("s1", 7, 1), ("q", 3, 1), ("s1", 7, 0), ("m", 0, 1), ("m", 1, 0), ("q", 4, 0), ("m", 1, 1), ("m", 2, 0), ("m", 2, 1), ("q", 4, 1), ("t", 0), ("m", 3, 0), ("q", 5, 0), ("m", 3, 1), ("m", 4, 0), ("q", 5, 1), ("t", 1), ("t", 2), ("m", 4, 1), ("m", 5, 0), ("q", 6, 0), ("q", 6, 1), ("t", 3), ("t", 4), ("m", 5, 1), ("q", 7, 0), ("q", 7, 1), ("m", 6, 0), ("m", 6, 1), ("m", 7, 0), ("m", 7, 1), ("t", 5), ("t", 6), ("t", 7)]
+        GPS = [("rd", 0, 0), ("rd", 1, 0), ("rd", 2, 0), ("rd", 3, 0), ("rd", 4, 0), ("rd", 5, 0), ("rd", 6, 0), ("rd", 7, 0)]
+        SYN = [("oR", 0), ("oR", 1), ("oR", 2), ("oR", 3), ("oR", 4), ("oy", 0), ("os", 0), ("oR", 5), ("oR", 6), ("oy", 1), ("os", 1), ("oR", 7), ("oy", 2), ("os", 2)]
+        table = {
+            "abs": absolute, "cos": cosine, "fac": factors, "fT": factor_turn, "fC": factor_copy,
+            "gv": lambda gk, ge: gup_copy(gk, ge, "V"), "gs": lambda gk, ge: gup_copy(gk, ge, "S"), "gq": gup_quant,
+            "s1": stage1, "pe": p_evac, "pv": p_evac_v, "pq": p_quant, "q": q_mm, "qe": q_evac, "m": m_mm, "pr": product, "rd": round_R,
+            "t": turn, "y": y_evac, "yq": y_quant, "oR": store_R, "oy": y_store, "os": s_store,
+            "fp": lambda k: times("fp", k), "fc": lambda k: times("fc", k),
+            "qfp": lambda k: quant_f("fp", k), "qfc": lambda k: quant_f("fc", k),
+            "rfp": lambda k: rows("fp", k), "rfc": lambda k: rows("fc", k),
+            "wfp": lambda k: weave_rows("fp", k), "wfc": lambda k: weave_rows("fc", k),
+        }
+        widths = [x for x in VEC if x[0] == "pq"]
 
-        def s1(dt):
-            stage1(dt, 0)
-            stage1(dt, 1)
+        def needs(x):
+            n, v = x[0], x[1:]
+            if n == "cos":
+                return [("abs", v[0])]
+            if n in ("fp", "fc"):
+                return [("cos", v[0]), ("fT", 1) if PSUM_FACTORS and (n, v[0]) not in ON_G else ("fac",)]
+            if n in ("rfp", "rfc"):
+                return [("cos", v[0]), ("fac",)]
+            if n in ("wfp", "wfc"):
+                return [("r" + n[1:], v[0])]
+            if n in ("qfp", "qfc"):
+                return [("w" + n[1:], v[0]) if (n[1:], v[0]) in ON_S else (n[1:], v[0])]
+            if n == "fT":
+                return [("fac",)] if v[0] == 0 else [("fC",)]
+            if n == "fC":
+                return [("fT", 0)]
+            if n == "gq":
+                return [("gv",) + v, ("gs",) + v]
+            if n == "s1":
+                return [("gq", 0, v[1]), ("gq", 1, v[1])]
+            if n in ("pe", "pv"):
+                return [("s1",) + v]
+            if n == "pq":
+                return [("pe", d, v[2]) if ("pe", d, v[2]) in SCA else ("pv", d, v[2]) for d in range(v[0], v[1])]
+            if n == "q":
+                return [w for w in widths if w[1] <= v[0] < w[2]]
+            if n == "qe":
+                return [("q",) + v]
+            if n == "m":
+                return [("qfc", v[0] // 2), ("qfc", 4 + v[0] // 2)] + [("qfp", 4 * g + 2 * v[1] + h) for g in range(2) for h in range(2)]
+            if n == "pr":
+                return [("m",) + v, ("qe",) + v]
+            if n == "rd":
+                return [("pr",) + v]
+            if n == "t":
+                return [("rd", v[0], 0), ("rd", v[0], 1)]
+            if n == "y":
+                return [("t", v[0])]
+            if n == "yq":
+                return [("y", d) for d in range(YG[v[0]][0], YG[v[0]][1])]
+            if n == "oR":
+                return [("pr", v[0], 0), ("pr", v[0], 1)]
+            if n in ("oy", "os"):
+                return [("yq", v[0], 0), ("yq", v[0], 1)]
+            return []
 
-        def pq(i):
-            p_quant(0, 256 * i, 256 * i + 256)
-            p_quant(1, 256 * i, 256 * i + 256)
-
-        def q2(dt):
-            q_mm(dt, 0)
-            q_mm(dt, 1)
-
-        pend = []
-
-        def unit(k, nm):
-            if nm == "t_fp":
-                times(k, r_f, nm)
-            else:
-                times(k, cr_f, nm)
-            flush(0)
-            pend.append((k, nm))
-
-        def flush(n):
-            while len(pend) > n:
-                k, nm = pend.pop(0)
-                if nm == "t_fp":
-                    quant_f(k, nm, fp_codes, fp_scales)
-                else:
-                    quant_f(k, nm, fc_codes, fc_scales)
-
-        evq = [("p", dt, h) for dt in range(4) for h in range(2)]
-        for i in range(3):
-            evq += [("q", dt, h) for dt in (2 * i, 2 * i + 1) for h in range(2)]
-            if i < 2:
-                evq += [("p", dt, h) for dt in (4 + 2 * i, 5 + 2 * i) for h in range(2)]
-        evq += [("q", dt, h) for dt in (6, 7) for h in range(2)]
-
-        def ev(n):
-            for unused in range(n):
-                if evq:
-                    what, dt, h = evq.pop(0)
-                    if what == "p":
-                        p_evac(dt, h)
-                    else:
-                        q_evac(dt, h)
-
-        pend.append((0, "t_fp"))
-        for dt in range(4):
-            s1(dt)
-        deferred = [2,6,3,7]
-        nev = [3,3,3,3,3,3,3,3]
-        absolute(2)
-        absolute(3)
-        for k in range(NCH):
-            if k > 0:
-                unit(k, "t_fp")
-            if 1 < k + 3 < NCH and k > 0:
-                absolute(k + 3)
-            if k not in deferred:
-                unit(k, "t_fc")
-            if k + 2 < NCH:
-                cosine(k + 2)
-            if k == 2:
-                pq(0)
-                q2(0)
-                q2(1)
-                s1(4)
-                s1(5)
-            if k == 3:
-                pq(1)
-                q2(2)
-                q2(3)
-                s1(6)
-                s1(7)
-            if k == 6:
-                pq(2)
-                q2(4)
-                q2(5)
-            ev(nev[k])
-        pq(3)
-        flush(0)
-
-        y_open(0)
-        y_open(1)
-
-        def mp(dt):
-            m_mm(dt, 0)
-            m_mm(dt, 1)
-
-        def out(dt):
-            product(dt)
-            store_R(dt)
-            round_R(dt)
-
-        def tr(dt):
-            turn(dt)
-            y_evac(dt)
-
-        late = [(2, "t_fc"), (6, "t_fc"), (3, "t_fc"), (7, "t_fc")]
-        mp(0)
-        mp(1)
-        q2(6)
-        q2(7)
-        product(0)
-        store_R(0)
-        if late:
-            unit(*late.pop(0))
-        product(1)
-        store_R(1)
-        if late:
-            unit(*late.pop(0))
-        flush(0)
-        ev(2)
-        round_R(0)
-        ev(2)
-        round_R(1)
-        ev(8)
-        mp(2)
-        tr(0)
-        tr(1)
-        mp(3)
-        out(2)
-        if late:
-            unit(*late.pop(0))
-        out(3)
-        if late:
-            unit(*late.pop(0))
-        flush(0)
-        mp(4)
-        tr(2)
-        tr(3)
-        mp(5)
-        out(4)
-        out(5)
-        y_quant(0, 0, 512)
-        y_store(0, 512)
-        mp(6)
-        tr(4)
-        tr(5)
-        mp(7)
-        out(6)
-        out(7)
-        y_quant(1, 0, 256)
-        tr(6)
-        tr(7)
-        y_quant(1, 256, 512)
-        y_store(512, 1024)
+        queues = [list(VEC), list(SCA), list(TEN), list(GPS), list(SYN)]
+        seen = set()
+        while any(queues):
+            moved = False
+            for qq in queues:
+                while qq and all(x in seen for x in needs(qq[0])):
+                    x = qq.pop(0)
+                    table[x[0]](*x[1:])
+                    seen.add(x)
+                    moved = True
+            assert moved, "no operation can go: %s" % [(qq[0], [x for x in needs(qq[0]) if x not in seen]) for qq in queues if qq]

@@ -21,12 +21,12 @@ G = 2
 P = 128
 CH = 256
 NCH = 8
-PSUM_FACTORS = False
-ON_G = []
-ON_S = []
+PSUM_FACTORS = True
+ON_G = [("fc", 1), ("fc", 5)]
+ON_S = [("fc", 7)]
 GS = 2
-YG = [[0,4],[4,6],[6,8]]
-RND = ["G","S"]
+YG = [[0,4],[4,6],[6,7],[7,8]]
+RND = [["G","G"],["G","G"],["G","G"],["G","G"],["G","G"],["G","S"],["G","S"],["G","S"]]
 
 
 def tile_kfrasinecurvaturepullback_x2_kernel(tc, w_words, w_scales, gup, a, r, c, out_0, out_1, out_2):
@@ -34,7 +34,7 @@ def tile_kfrasinecurvaturepullback_x2_kernel(tc, w_words, w_scales, gup, a, r, c
     with ExitStack() as ctx:
         keep = ctx.enter_context(tc.tile_pool(name="keep", bufs=1))
         stage = ctx.enter_context(tc.tile_pool(name="stage", bufs=3))
-        psum = ctx.enter_context(tc.psum_pool(name="psum", bufs=6))
+        psum = ctx.enter_context(tc.psum_pool(name="psum", bufs=5))
         psum_t = ctx.enter_context(tc.psum_pool(name="psum_t", bufs=2))
         psum_f = ctx.enter_context(tc.psum_pool(name="psum_f", bufs=1))
         ctx.enter_context(tc.manual_schedule())
@@ -42,7 +42,7 @@ def tile_kfrasinecurvaturepullback_x2_kernel(tc, w_words, w_scales, gup, a, r, c
         def made(pool, shape, dtype, name, tag=None, bufs=1):
             return pool.tile(shape, dtype, align_bytes=64, name=name, tag=tag or name, bufs=bufs)
 
-        a_cols = [[0,0,256],[0,256,512],[0,512,1024],[1,0,1024]]
+        a_cols = [[0,0,256],[0,256,512],[0,512,1024],[1,0,512],[1,512,1024]]
         a_sb = []
         for i, (g, c0, c1) in enumerate(a_cols):
             a_sb.append(made(keep, [P, 4, c1 - c0], BF16, "a%d" % i))
@@ -107,6 +107,7 @@ def tile_kfrasinecurvaturepullback_x2_kernel(tc, w_words, w_scales, gup, a, r, c
         load_g(1, 1)
         load_a(2)
         load_a(3)
+        load_a(4)
 
         ops = {}
 
@@ -115,7 +116,6 @@ def tile_kfrasinecurvaturepullback_x2_kernel(tc, w_words, w_scales, gup, a, r, c
                 ops[name] = (fn, needs)
             return put
 
-        t_abs = {}
         t_f = {}
         t_g = {}
         banks = {}
@@ -125,18 +125,19 @@ def tile_kfrasinecurvaturepullback_x2_kernel(tc, w_words, w_scales, gup, a, r, c
         y_codes = {}
         y_scales = {}
 
-        def absolute(k):
+        def absolute(i):
+            words = a_sb[i][:].rearrange("p t i -> p (t i)").bitcast(I32)
+            nc.vector.tensor_scalar(out=words, in0=words, scalar1=0x7FFF7FFF, scalar2=None, op0=ALU.bitwise_and)
+
+        def a_tile(k):
             g, c0 = k // 4, CH * (k % 4)
             for i, (ga, a0, a1) in enumerate(a_cols):
                 if ga == g and a0 <= c0 < a1:
-                    src = a_sb[i][:, :, c0 - a0 : c0 - a0 + CH]
-            t_abs[k] = made(stage, [P, 4, CH], BF16, "t_abs", None, 8)
-            nc.vector.tensor_scalar(
-                out=t_abs[k][:].bitcast(I32), in0=src.bitcast(I32), scalar1=0x7FFF7FFF, scalar2=None, op0=ALU.bitwise_and
-            )
+                    return i, c0 - a0
 
         def cosine(k):
-            nc.scalar.activation(out=cos_sb[:, k], in_=t_abs[k][:], func=ACT.Sin, scale=-1.0, bias=math.pi / 2)
+            i, c0 = a_tile(k)
+            nc.scalar.activation(out=cos_sb[:, k], in_=a_sb[i][:, :, c0 : c0 + CH], func=ACT.Sin, scale=-1.0, bias=math.pi / 2)
 
         def factors():
             nc.vector.tensor_copy(out=fac[:, 0:8], in_=r_bf[:])
@@ -153,8 +154,8 @@ def tile_kfrasinecurvaturepullback_x2_kernel(tc, w_words, w_scales, gup, a, r, c
             return where[:, c0 : c0 + 4]
 
         def times(nm, k):
-            tile = made(stage, [P, CH, 4], BF16, "t_f", None, 6)
             if (nm, k) in ON_G:
+                tile = made(stage, [P, CH, 4], BF16, "t_fg", None, 2)
                 for h in range(GS):
                     s = slice(CH // GS * h, CH // GS * h + CH // GS)
                     nc.gpsimd.tensor_tensor(
@@ -162,6 +163,7 @@ def tile_kfrasinecurvaturepullback_x2_kernel(tc, w_words, w_scales, gup, a, r, c
                         in1=factor(nm, k, fac).unsqueeze(1).broadcast_to([P, CH // GS, 4]), op=ALU.mult,
                     )
             else:
+                tile = made(stage, [P, CH, 4], BF16, "t_f", None, 6)
                 where = fac_ps[:, 1, :] if PSUM_FACTORS else fac
                 nc.vector.tensor_tensor(
                     out=tile[:].rearrange("p (c i) t -> p c t i", i=4),
@@ -171,7 +173,7 @@ def tile_kfrasinecurvaturepullback_x2_kernel(tc, w_words, w_scales, gup, a, r, c
             t_f[nm, k] = tile
 
         def rows(nm, k):
-            tile = made(stage, [P, 4, CH], BF16, "t_rows", None, 2)
+            tile = made(stage, [P, 4, CH], BF16, "t_rows", None, 1)
             for t in range(4):
                 c0 = (8 if nm == "fc" else 0) + 4 * (k // 4) + t
                 nc.vector.tensor_scalar(out=tile[:, t, :], in0=cos_sb[:, k, t, :], scalar1=fac[:, c0 : c0 + 1], scalar2=None, op0=ALU.mult)
@@ -276,44 +278,52 @@ def tile_kfrasinecurvaturepullback_x2_kernel(tc, w_words, w_scales, gup, a, r, c
                 t_Rb[dt] = made(stage, [P, 2, 2, P, 2], BF16, "t_Rb", None, 3)
             src = t_R[dt][:, 512 * h : 512 * h + 512].rearrange("p (m u e) -> p u m e", u=2, e=2)
             dst = t_Rb[dt][:, h]
-            if RND[h] == "G":
+            if RND[dt][h] == "G":
                 nc.gpsimd.tensor_scalar(out=dst, in0=src, scalar1=1.0, scalar2=1.0, op0=ALU.mult, op1=ALU.mult)
-            elif RND[h] == "V":
+            elif RND[dt][h] == "V":
                 nc.vector.tensor_copy(out=dst, in_=src)
             else:
                 nc.scalar.copy(out=dst, in_=src)
 
-        def turn(dt):
-            bank = psum_t.tile([P, 2, 2, P], F32, name="tbank")
+        def turn(dt, only=None):
+            if only != 1:
+                banks["t", dt] = psum_t.tile([P, 2, 2, P], F32, name="tbank")
+            bank = banks["t", dt]
             words = t_Rb[dt][:].rearrange("p g u m e -> p (g u m e)").bitcast(F32)
-            for g in range(G):
+            for g in range(G) if only is None else (only,):
                 for u in range(2):
                     k = 2 * g + u
                     nc.tensor.transpose(bank[:, g, u, :], words[:, 128 * k : 128 * k + 128], ident[:])
-            banks["t", dt] = bank
 
         def group(dt):
             for i, (d0, d1) in enumerate(YG):
                 if d0 <= dt < d1:
                     return i, d0, d1
 
-        def y_evac(dt):
+        def y_evac(dt, only=None):
             i, d0, d1 = group(dt)
             w = 128 * (d1 - d0)
             if i not in t_y:
-                t_y[i] = made(keep, [P, G, w, 4], BF16, "t_y%d" % i, "big" if w == 256 else None, 4 if w == 256 else 1)
+                t_y[i] = made(keep, [P, G, w, 4], BF16, "t_y%d" % i, "big" if w <= 256 else None, 4 if w <= 256 else 1)
             dst = t_y[i][:].rearrange("p g d t -> p (g d t)").bitcast(F32).rearrange("p (g d u) -> p g d u", g=G, u=2)
             s = slice(128 * (dt - d0), 128 * (dt - d0) + 128)
-            nc.scalar.copy(out=dst[:, :, s, :], in_=banks["t", dt][:].rearrange("p g u d -> p g d u"))
+            src = banks["t", dt][:].rearrange("p g u d -> p g d u")
+            if only is None:
+                nc.scalar.copy(out=dst[:, :, s, :], in_=src)
+            else:
+                nc.scalar.copy(out=dst[:, only, s, :], in_=src[:, only])
 
         def y_quant(i, g):
             d0, d1 = YG[i]
             w = 128 * (d1 - d0)
             if i not in y_codes:
                 y_codes[i] = made(keep, [P, G, w], U32, "y_codes%d" % i)
-                y_scales[i] = made(keep, [P, G, w], U8, "y_scales%d" % i)
+            half = d0 // 4
+            if half not in y_scales:
+                y_scales[half] = made(keep, [P, G, 512], U8, "y_scales%d" % half)
+            s0 = 128 * (d0 % 4)
             nc.vector.quantize_mx(
-                out=y_codes[i][:, g, :].bitcast(E4M3), scales=y_scales[i][:, g, :],
+                out=y_codes[i][:, g, :].bitcast(E4M3), scales=y_scales[half][:, g, s0 : s0 + w],
                 in_=t_y[i][:, g, :, :].rearrange("p d t -> p (d t)"),
             )
 
@@ -324,18 +334,18 @@ def tile_kfrasinecurvaturepullback_x2_kernel(tc, w_words, w_scales, gup, a, r, c
             )
 
         def s_store(i):
-            m0, m1 = 128 * YG[i][0], 128 * YG[i][1]
+            m0, m1 = 512 * i, 512 * i + 512
             for Q in range(4):
                 nc.sync.dma_start(
                     out=out_2[:, 4 * Q : 4 * Q + 4, m0:m1].rearrange("g q m -> q g m").bitcast(I32),
                     in_=y_scales[i][32 * Q : 32 * Q + 4, :, :].bitcast(I32),
                 )
 
-        VEC = [("abs", 0), ("gv", 0, 0), ("fac",), ("fc", 0), ("gv", 1, 0), ("fp", 0), ("abs", 1), ("gq", 1, 0), ("gv", 0, 1), ("qfp", 0), ("gq", 0, 0), ("gv", 1, 1), ("gq", 0, 1), ("abs", 2), ("abs", 3), ("gq", 1, 1), ("fp", 1), ("fp", 2), ("abs", 4), ("abs", 5), ("fc", 1), ("abs", 6), ("fp", 3), ("pq", 0, 2, 0), ("abs", 7), ("pq", 0, 2, 1), ("qfc", 0), ("fc", 4), ("qfp", 1), ("fp", 4), ("pq", 2, 4, 1), ("qfc", 1), ("qfp", 2), ("qfp", 3), ("fp", 5), ("pq", 2, 4, 0), ("fc", 5), ("qfp", 4), ("qfp", 5), ("qfc", 4), ("fp", 6), ("qfc", 5), ("fp", 7), ("qfp", 6), ("pq", 4, 6, 1), ("qfp", 7), ("fc", 2), ("pq", 4, 6, 0), ("pr", 0, 0), ("qfc", 2), ("pr", 0, 1), ("pr", 1, 0), ("fc", 6), ("fc", 3), ("qfc", 6), ("pr", 1, 1), ("pr", 2, 0), ("pr", 2, 1), ("pr", 3, 0), ("pr", 3, 1), ("pr", 4, 0), ("pq", 6, 8, 1), ("pq", 6, 8, 0), ("pr", 4, 1), ("pr", 5, 0), ("fc", 7), ("qfc", 3), ("qfc", 7), ("pr", 5, 1), ("yq", 0, 1), ("yq", 0, 0), ("pr", 6, 0), ("pr", 6, 1), ("pr", 7, 0), ("pr", 7, 1), ("yq", 1, 1), ("yq", 1, 0), ("yq", 2, 0), ("yq", 2, 1)]
-        SCA = [("cos", 0), ("gs", 1, 0), ("gs", 0, 0), ("cos", 1), ("gs", 0, 1), ("gs", 1, 1), ("pe", 0, 0), ("cos", 2), ("cos", 3), ("pe", 0, 1), ("pe", 1, 0), ("pe", 1, 1), ("cos", 4), ("pe", 2, 1), ("pe", 2, 0), ("pe", 3, 1), ("cos", 5), ("cos", 6), ("pe", 3, 0), ("pe", 4, 0), ("pe", 4, 1), ("qe", 0, 0), ("pe", 5, 0), ("qe", 0, 1), ("qe", 1, 0), ("cos", 7), ("pe", 5, 1), ("qe", 1, 1), ("qe", 2, 0), ("qe", 2, 1), ("pe", 6, 0), ("qe", 3, 0), ("pe", 6, 1), ("pe", 7, 1), ("qe", 3, 1), ("qe", 4, 0), ("pe", 7, 0), ("rd", 0, 1), ("y", 0), ("qe", 4, 1), ("qe", 5, 0), ("rd", 1, 1), ("rd", 2, 1), ("rd", 3, 1), ("y", 1), ("qe", 5, 1), ("y", 2), ("rd", 4, 1), ("qe", 6, 0), ("qe", 6, 1), ("y", 3), ("y", 4), ("qe", 7, 0), ("qe", 7, 1), ("rd", 5, 1), ("rd", 6, 1), ("y", 5), ("rd", 7, 1), ("y", 6), ("y", 7)]
-        TEN = [("s1", 0, 0), ("s1", 0, 1), ("s1", 1, 0), ("s1", 1, 1), ("s1", 2, 0), ("s1", 2, 1), ("s1", 3, 1), ("s1", 4, 1), ("s1", 3, 0), ("s1", 4, 0), ("q", 0, 0), ("s1", 5, 1), ("q", 0, 1), ("q", 1, 0), ("s1", 5, 0), ("s1", 6, 0), ("q", 1, 1), ("s1", 6, 1), ("q", 2, 0), ("q", 2, 1), ("q", 3, 0), ("m", 0, 0), ("s1", 7, 1), ("q", 3, 1), ("s1", 7, 0), ("m", 0, 1), ("m", 1, 0), ("q", 4, 0), ("m", 1, 1), ("m", 2, 0), ("m", 2, 1), ("q", 4, 1), ("t", 0), ("m", 3, 0), ("q", 5, 0), ("m", 3, 1), ("m", 4, 0), ("q", 5, 1), ("t", 1), ("t", 2), ("m", 4, 1), ("m", 5, 0), ("q", 6, 0), ("q", 6, 1), ("t", 3), ("t", 4), ("m", 5, 1), ("q", 7, 0), ("q", 7, 1), ("m", 6, 0), ("m", 6, 1), ("m", 7, 0), ("m", 7, 1), ("t", 5), ("t", 6), ("t", 7)]
-        GPS = [("rd", 0, 0), ("rd", 1, 0), ("rd", 2, 0), ("rd", 3, 0), ("rd", 4, 0), ("rd", 5, 0), ("rd", 6, 0), ("rd", 7, 0)]
-        SYN = [("oR", 0), ("oR", 1), ("oR", 2), ("oR", 3), ("oR", 4), ("oy", 0), ("os", 0), ("oR", 5), ("oR", 6), ("oy", 1), ("os", 1), ("oR", 7), ("oy", 2), ("os", 2)]
+        VEC = [("abs", 0), ("gv", 0, 0), ("fac",), ("gv", 1, 0), ("gq", 0, 0), ("fC",), ("gq", 1, 0), ("abs", 1), ("fc", 0), ("gv", 0, 1), ("fp", 0), ("gq", 0, 1), ("gv", 1, 1), ("abs", 2), ("qfp", 0), ("gq", 1, 1), ("qfc", 0), ("pq", 0, 2, 0), ("abs", 3), ("fp", 1), ("fp", 2), ("pq", 0, 2, 1), ("fp", 3), ("abs", 4), ("qfp", 1), ("qfp", 2), ("fp", 4), ("fc", 4), ("qfp", 3), ("qfc", 1), ("fp", 5), ("pq", 2, 4, 0), ("fp", 6), ("qfc", 4), ("qfp", 4), ("pq", 2, 4, 1), ("qfp", 5), ("qfc", 5), ("fp", 7), ("qfp", 6), ("qfp", 7), ("pr", 0, 0), ("pq", 4, 6, 1), ("pq", 4, 6, 0), ("pr", 0, 1), ("pr", 1, 0), ("pr", 1, 1), ("pr", 2, 0), ("fc", 2), ("fc", 6), ("qfc", 2), ("pq", 6, 8, 1), ("qfc", 6), ("pr", 2, 1), ("pq", 6, 8, 0), ("rfc", 7), ("pr", 3, 0), ("pr", 3, 1), ("fc", 3), ("pr", 4, 0), ("qfc", 3), ("qfc", 7), ("pr", 4, 1), ("pr", 5, 0), ("pr", 5, 1), ("pr", 6, 0), ("pr", 6, 1), ("yq", 0, 1), ("yq", 0, 0), ("pr", 7, 0), ("pr", 7, 1), ("yq", 1, 0), ("yq", 1, 1), ("yq", 2, 0), ("yq", 2, 1), ("yq", 3, 0), ("yq", 3, 1)]
+        SCA = [("gs", 0, 0), ("gs", 1, 0), ("cos", 0), ("pe", 0, 0), ("gs", 0, 1), ("gs", 1, 1), ("pe", 1, 0), ("cos", 1), ("cos", 2), ("cos", 3), ("pe", 0, 1), ("pe", 2, 0), ("pe", 1, 1), ("cos", 4), ("cos", 5), ("qe", 0, 0), ("pe", 3, 0), ("pe", 4, 0), ("cos", 6), ("pe", 2, 1), ("pe", 3, 1), ("pe", 4, 1), ("pe", 5, 1), ("qe", 0, 1), ("pe", 5, 0), ("cos", 7), ("pe", 6, 1), ("pe", 6, 0), ("qe", 1, 0), ("pe", 7, 0), ("qe", 1, 1), ("qe", 2, 0), ("qe", 2, 1), ("qe", 3, 0), ("pe", 7, 1), ("qe", 3, 1), ("qe", 4, 0), ("qe", 4, 1), ("y", 0), ("qe", 5, 0), ("wfc", 7), ("qe", 5, 1), ("y", 1), ("qe", 6, 0), ("y", 2), ("qe", 6, 1), ("qe", 7, 0), ("rd", 5, 1), ("y", 3), ("rd", 6, 1), ("y", 4), ("y", 5), ("qe", 7, 1), ("y", 6), ("rd", 7, 1), ("y", 7, 0), ("y", 7, 1)]
+        TEN = [("fT", 0), ("fT", 1), ("s1", 0, 0), ("s1", 1, 0), ("s1", 2, 0), ("s1", 0, 1), ("s1", 1, 1), ("s1", 3, 0), ("s1", 4, 0), ("s1", 2, 1), ("q", 0, 0), ("s1", 3, 1), ("s1", 4, 1), ("s1", 5, 1), ("s1", 5, 0), ("q", 0, 1), ("q", 1, 0), ("s1", 6, 1), ("s1", 6, 0), ("s1", 7, 0), ("s1", 7, 1), ("q", 1, 1), ("m", 0, 0), ("q", 2, 0), ("q", 2, 1), ("m", 0, 1), ("m", 1, 0), ("m", 1, 1), ("m", 2, 0), ("q", 3, 0), ("t", 0), ("q", 3, 1), ("q", 4, 0), ("q", 4, 1), ("q", 5, 0), ("m", 2, 1), ("q", 5, 1), ("m", 3, 0), ("m", 3, 1), ("m", 4, 0), ("m", 4, 1), ("m", 5, 0), ("t", 1), ("t", 2), ("q", 6, 0), ("q", 6, 1), ("m", 5, 1), ("q", 7, 0), ("m", 6, 0), ("m", 6, 1), ("t", 3), ("t", 4), ("m", 7, 0), ("t", 5), ("q", 7, 1), ("m", 7, 1), ("t", 6), ("t", 7, 0), ("t", 7, 1)]
+        GPS = [("fc", 1), ("fc", 5), ("rd", 0, 0), ("rd", 0, 1), ("rd", 1, 0), ("rd", 1, 1), ("rd", 2, 0), ("rd", 2, 1), ("rd", 3, 0), ("rd", 4, 0), ("rd", 3, 1), ("rd", 4, 1), ("rd", 5, 0), ("rd", 6, 0), ("rd", 7, 0)]
+        SYN = [("oR", 0), ("oR", 1), ("oR", 2), ("oR", 3), ("oR", 4), ("oy", 0), ("os", 0), ("oR", 5), ("oy", 1), ("oR", 6), ("oy", 2), ("oR", 7), ("oy", 3), ("os", 1)]
         table = {
             "abs": absolute, "cos": cosine, "fac": factors, "fT": factor_turn, "fC": factor_copy,
             "gv": lambda gk, ge: gup_copy(gk, ge, "V"), "gs": lambda gk, ge: gup_copy(gk, ge, "S"), "gq": gup_quant,
@@ -351,7 +361,7 @@ def tile_kfrasinecurvaturepullback_x2_kernel(tc, w_words, w_scales, gup, a, r, c
         def needs(x):
             n, v = x[0], x[1:]
             if n == "cos":
-                return [("abs", v[0])]
+                return [("abs", a_tile(v[0])[0])]
             if n in ("fp", "fc"):
                 return [("cos", v[0]), ("fT", 1) if PSUM_FACTORS and (n, v[0]) not in ON_G else ("fac",)]
             if n in ("rfp", "rfc"):
@@ -383,15 +393,17 @@ def tile_kfrasinecurvaturepullback_x2_kernel(tc, w_words, w_scales, gup, a, r, c
             if n == "rd":
                 return [("pr",) + v]
             if n == "t":
-                return [("rd", v[0], 0), ("rd", v[0], 1)]
+                return [("rd", v[0], 0), ("rd", v[0], 1)] if len(v) == 1 else [("rd",) + v]
             if n == "y":
-                return [("t", v[0])]
+                return [("t",) + v]
             if n == "yq":
-                return [("y", d) for d in range(YG[v[0]][0], YG[v[0]][1])]
+                return [("y", d) if ("y", d) in SCA else ("y", d, v[1]) for d in range(YG[v[0]][0], YG[v[0]][1])]
             if n == "oR":
                 return [("pr", v[0], 0), ("pr", v[0], 1)]
-            if n in ("oy", "os"):
+            if n == "oy":
                 return [("yq", v[0], 0), ("yq", v[0], 1)]
+            if n == "os":
+                return [("yq", i, g) for i in range(len(YG)) if YG[i][0] // 4 == v[0] for g in range(G)]
             return []
 
         queues = [list(VEC), list(SCA), list(TEN), list(GPS), list(SYN)]

@@ -15,405 +15,395 @@ E2M1 = mybir.dt.float4_e2m1fn_x4
 ALU = mybir.AluOpType
 ACT = mybir.ActivationFunctionType
 
-N = 1024
-FLOPS = 3 * 2 * N * N * N
-G = 2
 P = 128
-CH = 256
-NCH = 8
-PSUM_FACTORS = True
-ON_G = [("fc", 1), ("fc", 5)]
-ON_S = [("fc", 7)]
-GS = 2
-YG = [[0,4],[4,6],[6,7],[7,8]]
-RND = [["G","G"],["G","G"],["G","G"],["G","G"],["G","G"],["G","S"],["G","S"],["G","S"]]
+N = 1024
+GROUPS = 2
+TILES = 8
+CHUNK = 256
+CHUNKS = 8
+FLOPS = 3 * 2 * N * N * N
+
+A_PARTS = ((0, 0, 256), (0, 256, 512), (0, 512, 1024), (1, 0, 512), (1, 512, 1024))
+
+Y_SETS = ((0, 4), (4, 6), (6, 7), (7, 8))
+
+VECTOR = """
+abs gup_lo fc fp gup_lo abs gup_q*2 gup_lo fc gup_q gup_lo abs gup_q fp abs p_q fp_q fp*3 fc_q fc p_q fc abs
+fp p_q*2 fc_q fp_q*2 fp*2 p_q fp_q product fc product*2 p_q fc product*2 fc product fc fc_q*2 product*3
+p_q*2 product*3 y_q*2 product*3 y_q*2 product y_q*4
+"""
+SCALAR = """
+sine gup_hi*2 sine gup_hi*2 p_copy*2 sine*4 p_copy*8 q_copy p_copy q_copy sine*2 p_copy*2 q_copy*2 p_copy
+q_copy*3 round_hi p_copy y_copy round_hi q_copy*2 round_hi q_copy*2 p_copy y_copy*2 round_hi q_copy y_copy
+round_hi q_copy round_hi q_copy*2 y_copy*2 round_hi q_copy y_copy round_hi y_copy*2
+"""
+TENSOR = """
+p*11 q*4 p*3 m q*3 p m*5 turn q*3 m q p m turn*2 q m*4 turn m q*2 m q turn*2 m q m turn*3
+"""
+GPSIMD = "factors round_lo*8"
+SYNC = "store_out*5 store_codes store_scales store_out store_codes store_out store_codes store_out store_codes store_scales"
+
+PAIRS = [(a, b) for a in range(TILES) for b in range(2)]
+GUP_PARTS = [(0, 0), (1, 0), (0, 1), (1, 1)]
+P_PARTS = [(0, 0)] + [(d + 1 - g, g) for d in range(TILES - 1) for g in range(2)] + [(TILES - 1, 1)]
+FC_CHUNKS = [(0,), (1,), (4,), (5,), (2,), (3,), (6,), (7,)]
+TURNS = [(d, (0, 1)) for d in range(TILES - 1)] + [(TILES - 1, (0,)), (TILES - 1, (1,))]
+
+STREAMS = {
+    "abs": [(i,) for i in range(len(A_PARTS))],
+    "sine": [(i,) for i in range(CHUNKS)],
+    "factors": [()],
+    "fp": [(i,) for i in range(CHUNKS)],
+    "fc": FC_CHUNKS,
+    "fp_q": [(i,) for i in range(0, CHUNKS, 2)],
+    "fc_q": FC_CHUNKS[::2],
+    "gup_lo": GUP_PARTS,
+    "gup_hi": GUP_PARTS,
+    "gup_q": GUP_PARTS,
+    "p": P_PARTS,
+    "p_copy": P_PARTS,
+    "p_q": [(d, g) for d in range(0, TILES, 2) for g in range(GROUPS)],
+    "q": PAIRS,
+    "q_copy": PAIRS,
+    "m": PAIRS,
+    "product": PAIRS,
+    "round_lo": [(d,) for d in range(TILES)],
+    "round_hi": [(d,) for d in range(TILES)],
+    "turn": TURNS,
+    "y_copy": TURNS,
+    "y_q": [(i, g) for i in range(len(Y_SETS)) for g in range(GROUPS)],
+    "store_out": [(d,) for d in range(TILES)],
+    "store_codes": [(i,) for i in range(len(Y_SETS))],
+    "store_scales": [(h,) for h in range(2)],
+}
+
+
+def a_part(chunk):
+    group, col = chunk // 4, CHUNK * (chunk % 4)
+    for i, (g, c0, c1) in enumerate(A_PARTS):
+        if g == group and c0 <= col < c1:
+            return i, col - c0
+
+
+def y_set(tile):
+    return [i for i, (d0, d1) in enumerate(Y_SETS) if d0 <= tile < d1][0]
+
+
+NEEDS = {
+    "sine": lambda i: [("abs", a_part(i)[0])],
+    "fp": lambda i: [("sine", i), ("factors",)],
+    "fc": lambda i: [("sine", i), ("factors",)],
+    "fp_q": lambda i: [("fp", i), ("fp", i + 1)],
+    "fc_q": lambda i: [("fc", i), ("fc", i + 1)],
+    "gup_q": lambda k, e: [("gup_lo", k, e), ("gup_hi", k, e)],
+    "p": lambda d, e: [("gup_q", 0, e), ("gup_q", 1, e)],
+    "p_copy": lambda d, e: [("p", d, e)],
+    "p_q": lambda d, e: [("p_copy", d, e), ("p_copy", d + 1, e)],
+    "q": lambda d, h: [("p_q", d // 2 * 2, e) for e in range(GROUPS)],
+    "q_copy": lambda d, h: [("q", d, h)],
+    "m": lambda d, h: [(s, 4 * g + 2 * c) for g in range(GROUPS) for s, c in (("fc_q", d // 4), ("fp_q", h))],
+    "product": lambda d, h: [("m", d, h), ("q_copy", d, h)],
+    "round_lo": lambda d: [("product", d, 0)],
+    "round_hi": lambda d: [("product", d, 1)],
+    "turn": lambda d, halves: [(("round_lo", "round_hi")[h], d) for h in halves],
+    "y_copy": lambda d, halves: [("turn", d, halves)],
+    "y_q": lambda i, g: [("y_copy",) + t for t in TURNS if y_set(t[0]) == i and g in t[1]],
+    "store_out": lambda d: [("product", d, 0), ("product", d, 1)],
+    "store_codes": lambda i: [("y_q", i, g) for g in range(GROUPS)],
+    "store_scales": lambda h: [("y_q", i, g) for i in range(len(Y_SETS)) if Y_SETS[i][0] // 4 == h for g in range(GROUPS)],
+}
+
+
+def calls_of(orders):
+    streams = {stage: list(calls) for stage, calls in STREAMS.items()}
+    lists = []
+    for order in orders:
+        calls = []
+        for run in order.split():
+            stage, count = (run.split("*") + ["1"])[:2]
+            for i in range(int(count)):
+                calls.append((stage,) + streams[stage].pop(0))
+        lists.append(calls)
+    return lists
 
 
 def tile_kfrasinecurvaturepullback_x2_kernel(tc, w_words, w_scales, gup, a, r, c, out_0, out_1, out_2):
     nc = tc.nc
     with ExitStack() as ctx:
         keep = ctx.enter_context(tc.tile_pool(name="keep", bufs=1))
-        stage = ctx.enter_context(tc.tile_pool(name="stage", bufs=3))
-        psum = ctx.enter_context(tc.psum_pool(name="psum", bufs=5))
-        psum_t = ctx.enter_context(tc.psum_pool(name="psum_t", bufs=2))
-        psum_f = ctx.enter_context(tc.psum_pool(name="psum_f", bufs=1))
+        stage_pool = ctx.enter_context(tc.tile_pool(name="stage", bufs=3))
+        psum = ctx.enter_context(tc.psum_pool(name="psum", bufs=6))
+        psum_turn = ctx.enter_context(tc.psum_pool(name="psum_turn", bufs=2))
         ctx.enter_context(tc.manual_schedule())
 
-        def made(pool, shape, dtype, name, tag=None, bufs=1):
+        def new(pool, shape, dtype, name, tag=None, bufs=1):
             return pool.tile(shape, dtype, align_bytes=64, name=name, tag=tag or name, bufs=bufs)
 
-        a_cols = [[0,0,256],[0,256,512],[0,512,1024],[1,0,512],[1,512,1024]]
         a_sb = []
-        for i, (g, c0, c1) in enumerate(a_cols):
-            a_sb.append(made(keep, [P, 4, c1 - c0], BF16, "a%d" % i))
-        g_raw = {}
-        for gk in range(G):
-            for ge in range(G):
-                g_raw[gk, ge] = made(keep, [P, 4, 512], BF16, "g_raw%d%d" % (gk, ge), "big", 4)
-        w_sb = made(keep, [P, G, 2 * N], U8, "w_sb")
-        ws_sb = made(keep, [P, G, N], U8, "ws_sb")
-        r_bf = made(keep, [P, G * 4], BF16, "r_bf")
-        c_bf = made(keep, [P, G * 4], BF16, "c_bf")
-        ident = made(keep, [P, P], F32, "ident")
-        fac = made(keep, [P, P], F32, "fac")
-        g_codes = made(keep, [P, G, N], U32, "g_codes")
-        g_scales = made(keep, [P, G, N], U8, "g_scales")
-        fp_codes = made(keep, [P, G, N], U32, "fp_codes")
-        fp_scales = made(keep, [P, G, N], U8, "fp_scales")
-        fc_codes = made(keep, [P, G, N], U32, "fc_codes")
-        fc_scales = made(keep, [P, G, N], U8, "fc_scales")
-        cos_sb = made(keep, [P, NCH, 4, CH], F32, "cos_sb")
-        p_bf = made(keep, [P, G, N, 4], BF16, "p_bf")
-        p_codes = made(keep, [P, G, N], U32, "p_codes")
-        p_scales = made(keep, [P, G, N], U8, "p_scales")
-        q_sb = made(keep, [P, 8, N], F32, "q_sb")
-        if PSUM_FACTORS:
-            fac_t = made(keep, [P, P], F32, "fac_t")
-            fac_ps = psum_f.tile([P, 2, P], F32, name="fac_ps")
-
-        nc.vector.memset(ws_sb[:].rearrange("p g n -> p (g n)").bitcast(I32), 0)
-        if PSUM_FACTORS:
-            nc.gpsimd.memset(fac[:], 0.0)
+        for i, (g, c0, c1) in enumerate(A_PARTS):
+            a_sb.append(new(keep, [P, 4, c1 - c0], BF16, "a%d" % i))
+        gup_sb = {}
+        for k, e in GUP_PARTS:
+            gup_sb[k, e] = new(keep, [P, 4, 512], BF16, "gup%d%d" % (k, e), "raw", 4)
+        w_sb = new(keep, [P, GROUPS, 2 * N], U8, "w_sb")
+        w_sc = new(keep, [P, GROUPS, N], U8, "w_sc")
+        r_bf = new(keep, [P, 4 * GROUPS], BF16, "r_bf")
+        c_bf = new(keep, [P, 4 * GROUPS], BF16, "c_bf")
+        ident = new(keep, [P, P], F32, "ident")
+        r_f = new(keep, [P, 4 * GROUPS], F32, "r_f")
+        cr_f = new(keep, [P, 4 * GROUPS], F32, "cr_f")
+        gup_codes = new(keep, [P, GROUPS, N], U32, "gup_codes")
+        gup_sc = new(keep, [P, GROUPS, N], U8, "gup_sc")
+        fp_codes = new(keep, [P, GROUPS, N], U32, "fp_codes")
+        fp_sc = new(keep, [P, GROUPS, N], U8, "fp_sc")
+        fc_codes = new(keep, [P, GROUPS, N], U32, "fc_codes")
+        fc_sc = new(keep, [P, GROUPS, N], U8, "fc_sc")
+        cos_sb = new(keep, [P, CHUNKS, 4, CHUNK], F32, "cos_sb")
+        p_bf = new(keep, [P, GROUPS, N, 4], BF16, "p_bf")
+        p_codes = new(keep, [P, GROUPS, N], U32, "p_codes")
+        p_sc = new(keep, [P, GROUPS, N], U8, "p_sc")
+        q_sb = new(keep, [P, TILES, N], F32, "q_sb")
+        a_abs, gup_il, f_il, bank, out_sb, out_bf, y_il, y_codes, y_sc = {}, {}, {}, {}, {}, {}, {}, {}, {}
 
         def load_a(i):
-            g, c0, c1 = a_cols[i]
+            g, c0, c1 = A_PARTS[i]
             nc.sync.dma_start(out=a_sb[i][:], in_=a[512 * g : 512 * g + 512, c0:c1].rearrange("(p t) i -> p t i", t=4))
 
-        def load_g(gk, ge):
-            nc.sync.dma_start(
-                out=g_raw[gk, ge][:], in_=gup[512 * gk : 512 * gk + 512, 512 * ge : 512 * ge + 512].rearrange("(p t) e -> p t e", t=4)
-            )
+        def load_gup(k, e):
+            rows, cols = slice(512 * k, 512 * k + 512), slice(512 * e, 512 * e + 512)
+            nc.sync.dma_start(out=gup_sb[k, e][:], in_=gup[rows, cols].rearrange("(p t) e -> p t e", t=4))
 
-        def load_w():
-            nc.sync.dma_start(out=w_sb[:].bitcast(I32), in_=w_words.rearrange("g p n -> p g n").bitcast(I32))
-
-        def load_ws(eng):
-            for Q in range(4):
-                eng.dma_start(
-                    out=ws_sb[32 * Q : 32 * Q + 4, :, :].bitcast(I32),
-                    in_=w_scales[:, 4 * Q : 4 * Q + 4, :].rearrange("g q n -> q g n").bitcast(I32),
-                )
-
-        nc.gpsimd.dma_start(out=r_bf[:].rearrange("p (g t) -> p g t", g=G), in_=r.rearrange("(g p t) -> p g t", g=G, t=4))
-        nc.gpsimd.dma_start(out=c_bf[:].rearrange("p (g t) -> p g t", g=G), in_=c.rearrange("(g p t) -> p g t", g=G, t=4))
+        nc.vector.memset(w_sc[:].rearrange("p g n -> p (g n)").bitcast(I32), 0)
         make_identity(nc, ident[:])
         load_a(0)
-        load_g(0, 0)
-        load_ws(nc.sync)
-        load_g(1, 0)
-        load_w()
+        load_gup(0, 0)
+        for vec, tile in ((r, r_bf), (c, c_bf)):
+            nc.sync.dma_start(
+                out=tile[:].rearrange("p (g t) -> p g t", g=GROUPS), in_=vec.rearrange("(g p t) -> p g t", g=GROUPS, t=4)
+            )
+        load_gup(1, 0)
+        nc.sync.dma_start(out=w_sb[:].bitcast(I32), in_=w_words.rearrange("g p n -> p g n").bitcast(I32))
+        for quad in range(4):
+            nc.sync.dma_start(
+                out=w_sc[32 * quad : 32 * quad + 4, :, :].bitcast(I32),
+                in_=w_scales[:, 4 * quad : 4 * quad + 4, :].rearrange("g s n -> s g n").bitcast(I32),
+            )
         load_a(1)
-        load_g(0, 1)
-        load_g(1, 1)
+        load_gup(0, 1)
+        load_gup(1, 1)
         load_a(2)
         load_a(3)
         load_a(4)
 
-        ops = {}
-
-        def op(name, needs):
-            def put(fn):
-                ops[name] = (fn, needs)
-            return put
-
-        t_f = {}
-        t_g = {}
-        banks = {}
-        t_R = {}
-        t_Rb = {}
-        t_y = {}
-        y_codes = {}
-        y_scales = {}
-
         def absolute(i):
-            words = a_sb[i][:].rearrange("p t i -> p (t i)").bitcast(I32)
-            nc.vector.tensor_scalar(out=words, in0=words, scalar1=0x7FFF7FFF, scalar2=None, op0=ALU.bitwise_and)
+            width = A_PARTS[i][2] - A_PARTS[i][1]
+            a_abs[i] = new(stage_pool, [P, 4, width], BF16, "a_abs", None, 3)
+            nc.vector.tensor_scalar(
+                out=a_abs[i][:].rearrange("p t i -> p (t i)").bitcast(I32),
+                in0=a_sb[i][:].rearrange("p t i -> p (t i)").bitcast(I32),
+                scalar1=0x7FFF7FFF, scalar2=None, op0=ALU.bitwise_and,
+            )
 
-        def a_tile(k):
-            g, c0 = k // 4, CH * (k % 4)
-            for i, (ga, a0, a1) in enumerate(a_cols):
-                if ga == g and a0 <= c0 < a1:
-                    return i, c0 - a0
-
-        def cosine(k):
-            i, c0 = a_tile(k)
-            nc.scalar.activation(out=cos_sb[:, k], in_=a_sb[i][:, :, c0 : c0 + CH], func=ACT.Sin, scale=-1.0, bias=math.pi / 2)
+        def sine(i):
+            part, c0 = a_part(i)
+            nc.scalar.activation(
+                out=cos_sb[:, i], in_=a_abs[part][:, :, c0 : c0 + CHUNK], func=ACT.Sin, scale=-1.0, bias=math.pi / 2
+            )
 
         def factors():
-            nc.vector.tensor_copy(out=fac[:, 0:8], in_=r_bf[:])
-            nc.vector.tensor_tensor(out=fac[:, 8:16], in0=c_bf[:], in1=r_bf[:], op=ALU.mult)
+            nc.gpsimd.tensor_copy(out=r_f[:], in_=r_bf[:])
+            nc.gpsimd.tensor_tensor(out=cr_f[:], in0=c_bf[:], in1=r_bf[:], op=ALU.mult)
 
-        def factor_turn(i):
-            nc.tensor.transpose(fac_ps[:, i, :], (fac, fac_t)[i][:], ident[:])
+        def times(name, factor, i):
+            if (name, i // 2) not in f_il:
+                f_il[name, i // 2] = new(stage_pool, [P, 2 * CHUNK, 4], BF16, "f_il", None, 3)
+            half = slice(CHUNK * (i % 2), CHUNK * (i % 2) + CHUNK)
+            g = i // 4
+            nc.vector.tensor_tensor(
+                out=f_il[name, i // 2][:, half, :].rearrange("p (c i) t -> p c t i", i=4),
+                in0=cos_sb[:, i].rearrange("p t (c i) -> p c t i", i=4),
+                in1=factor[:, 4 * g : 4 * g + 4].unsqueeze(1).unsqueeze(3).broadcast_to([P, CHUNK // 4, 4, 4]),
+                op=ALU.mult,
+            )
 
-        def factor_copy():
-            nc.vector.tensor_copy(out=fac_t[:], in_=fac_ps[:, 0, :])
+        def quantise_f(name, codes, scales, i):
+            g, cols = i // 4, slice(CHUNK * (i % 4), CHUNK * (i % 4) + 2 * CHUNK)
+            nc.vector.quantize_mx(
+                out=codes[:, g, cols].bitcast(E4M3), scales=scales[:, g, cols],
+                in_=f_il[name, i // 2][:].rearrange("p i t -> p (i t)"),
+            )
 
-        def factor(nm, k, where):
-            c0 = (8 if nm == "fc" else 0) + 4 * (k // 4)
-            return where[:, c0 : c0 + 4]
-
-        def times(nm, k):
-            if (nm, k) in ON_G:
-                tile = made(stage, [P, CH, 4], BF16, "t_fg", None, 2)
-                for h in range(GS):
-                    s = slice(CH // GS * h, CH // GS * h + CH // GS)
-                    nc.gpsimd.tensor_tensor(
-                        out=tile[:, s, :], in0=cos_sb[:, k, :, s].rearrange("p t i -> p i t"),
-                        in1=factor(nm, k, fac).unsqueeze(1).broadcast_to([P, CH // GS, 4]), op=ALU.mult,
-                    )
+        def interleave_gup(engine, k, e):
+            if (k, e) not in gup_il:
+                gup_il[k, e] = new(stage_pool, [P, 4, P, 4], BF16, "gup_il", "row", 4)
+            t = slice(0, 2) if engine == "vector" else slice(2, 4)
+            src = gup_sb[k, e][:].rearrange("p j (m t) -> p t m j", t=4)
+            if engine == "vector":
+                nc.vector.tensor_copy(out=gup_il[k, e][:, t], in_=src[:, t])
             else:
-                tile = made(stage, [P, CH, 4], BF16, "t_f", None, 6)
-                where = fac_ps[:, 1, :] if PSUM_FACTORS else fac
-                nc.vector.tensor_tensor(
-                    out=tile[:].rearrange("p (c i) t -> p c t i", i=4),
-                    in0=cos_sb[:, k].rearrange("p t (c i) -> p c t i", i=4),
-                    in1=factor(nm, k, where).unsqueeze(1).unsqueeze(3).broadcast_to([P, CH // 4, 4, 4]), op=ALU.mult,
-                )
-            t_f[nm, k] = tile
+                nc.scalar.copy(out=gup_il[k, e][:, t], in_=src[:, t])
 
-        def rows(nm, k):
-            tile = made(stage, [P, 4, CH], BF16, "t_rows", None, 1)
-            for t in range(4):
-                c0 = (8 if nm == "fc" else 0) + 4 * (k // 4) + t
-                nc.vector.tensor_scalar(out=tile[:, t, :], in0=cos_sb[:, k, t, :], scalar1=fac[:, c0 : c0 + 1], scalar2=None, op0=ALU.mult)
-            t_f[nm + "m", k] = tile
-
-        def weave_rows(nm, k):
-            tile = made(stage, [P, CH, 4], BF16, "t_f", None, 6)
-            nc.scalar.copy(out=tile[:].rearrange("p (c i) t -> p c t i", i=4), in_=t_f[nm + "m", k][:].rearrange("p t (c i) -> p c t i", i=4))
-            t_f[nm, k] = tile
-
-        def quant_f(nm, k):
-            g, c0 = k // 4, CH * (k % 4)
-            codes, scales = (fp_codes, fp_scales) if nm == "fp" else (fc_codes, fc_scales)
+        def quantise_gup(k, e):
+            cols = slice(512 * e, 512 * e + 512)
             nc.vector.quantize_mx(
-                out=codes[:, g, c0 : c0 + CH].bitcast(E4M3), scales=scales[:, g, c0 : c0 + CH],
-                in_=t_f[nm, k][:].rearrange("p i t -> p (i t)"),
+                out=gup_codes[:, k, cols].bitcast(E4M3), scales=gup_sc[:, k, cols],
+                in_=gup_il[k, e][:].rearrange("p t m j -> p (t m j)"),
             )
 
-        def gup_copy(gk, ge, eng):
-            if (gk, ge) not in t_g:
-                t_g[gk, ge] = made(stage, [P, 4, P, 4], BF16, "t_g", "k4", 4)
-            src = g_raw[gk, ge][:].rearrange("p j (m t) -> p t m j", t=4)
-            dst = t_g[gk, ge]
-            v = {(0, 0): 2, (1, 0): 2, (0, 1): 2, (1, 1): 2}[gk, ge]
-            if eng == "V" and v > 0:
-                nc.vector.tensor_copy(out=dst[:, 0:v], in_=src[:, 0:v])
-            if eng == "S" and v < 4:
-                nc.scalar.copy(out=dst[:, v:4], in_=src[:, v:4])
-
-        def gup_quant(gk, ge):
-            nc.vector.quantize_mx(
-                out=g_codes[:, gk, 512 * ge : 512 * ge + 512].bitcast(E4M3), scales=g_scales[:, gk, 512 * ge : 512 * ge + 512],
-                in_=t_g[gk, ge][:].rearrange("p t m j -> p (t m j)"),
-            )
-
-        def stage1(dt, ge):
-            bank = psum.tile([P, 512], F32, name="bank")
+        def p_matmul(d, e):
+            bank["p", d, e] = psum.tile([P, 512], F32, name="bank")
             for t in range(4):
-                for gk in range(G):
-                    e0 = 512 * ge + 128 * t
+                cols = slice(512 * e + 128 * t, 512 * e + 128 * t + 128)
+                for k in range(GROUPS):
                     nc.tensor.matmul_mx(
-                        out=bank[:, 128 * t : 128 * t + 128],
-                        lhsT=g_codes[:, gk, e0 : e0 + 128].bitcast(E4M3), lhsT_scale=g_scales[:, gk, e0 : e0 + 128],
-                        rhs=w_sb[:, gk, 256 * dt : 256 * dt + 256].bitcast(E2M1), rhs_scale=ws_sb[:, gk, 128 * dt : 128 * dt + 128],
-                        start=(gk == 0), stop=(gk == 1),
+                        out=bank["p", d, e][:, 128 * t : 128 * t + 128],
+                        lhsT=gup_codes[:, k, cols].bitcast(E4M3), lhsT_scale=gup_sc[:, k, cols],
+                        rhs=w_sb[:, k, 256 * d : 256 * d + 256].bitcast(E2M1), rhs_scale=w_sc[:, k, 128 * d : 128 * d + 128],
+                        start=(k == 0), stop=(k == GROUPS - 1),
                     )
-            banks["p", dt, ge] = bank
 
-        def p_evac(dt, ge):
-            dst = p_bf[:, ge, 128 * dt : 128 * dt + 128, :]
-            src = banks["p", dt, ge][:].rearrange("p (t d) -> p d t", t=4)
-            nc.scalar.copy(out=dst, in_=src)
-
-        def p_evac_v(dt, ge):
-            dst = p_bf[:, ge, 128 * dt : 128 * dt + 128, :]
-            src = banks["p", dt, ge][:].rearrange("p (t d) -> p d t", t=4)
-            nc.vector.tensor_copy(out=dst, in_=src)
-
-        def p_quant(d0, d1, ge):
-            s = slice(128 * d0, 128 * d1)
-            nc.vector.quantize_mx(
-                out=p_codes[:, ge, s].bitcast(E4M3), scales=p_scales[:, ge, s],
-                in_=p_bf[:, ge, s, :].rearrange("p d t -> p (d t)"),
+        def p_copy(d, e):
+            nc.scalar.copy(
+                out=p_bf[:, e, 128 * d : 128 * d + 128, :], in_=bank["p", d, e][:].rearrange("p (t d) -> p d t", t=4)
             )
 
-        def q_mm(dt, jh):
-            bank = psum.tile([P, 512], F32, name="bank")
-            for ge in range(G):
+        def quantise_p(d, e):
+            rows = slice(128 * d, 128 * d + 256)
+            nc.vector.quantize_mx(
+                out=p_codes[:, e, rows].bitcast(E4M3), scales=p_sc[:, e, rows],
+                in_=p_bf[:, e, rows, :].rearrange("p d t -> p (d t)"),
+            )
+
+        def q_matmul(d, h):
+            rows, cols = slice(128 * d, 128 * d + 128), slice(512 * h, 512 * h + 512)
+            bank["q", d, h] = psum.tile([P, 512], F32, name="bank")
+            for e in range(GROUPS):
                 nc.tensor.matmul_mx(
-                    out=bank[:],
-                    lhsT=p_codes[:, ge, 128 * dt : 128 * dt + 128].bitcast(E4M3), lhsT_scale=p_scales[:, ge, 128 * dt : 128 * dt + 128],
-                    rhs=w_sb[:, ge, 1024 * jh : 1024 * jh + 1024].bitcast(E2M1), rhs_scale=ws_sb[:, ge, 512 * jh : 512 * jh + 512],
-                    start=(ge == 0), stop=(ge == 1),
+                    out=bank["q", d, h][:],
+                    lhsT=p_codes[:, e, rows].bitcast(E4M3), lhsT_scale=p_sc[:, e, rows],
+                    rhs=w_sb[:, e, 1024 * h : 1024 * h + 1024].bitcast(E2M1), rhs_scale=w_sc[:, e, cols],
+                    start=(e == 0), stop=(e == GROUPS - 1),
                 )
-            banks["q", dt, jh] = bank
 
-        def q_evac(dt, jh):
-            nc.scalar.activation(out=q_sb[:, dt, 512 * jh : 512 * jh + 512], in_=banks["q", dt, jh][:], func=ACT.Copy, scale=1.0 / N)
+        def q_copy(d, h):
+            nc.scalar.activation(
+                out=q_sb[:, d, 512 * h : 512 * h + 512], in_=bank["q", d, h][:], func=ACT.Copy, scale=1.0 / N
+            )
 
-        def m_mm(dt, jh):
-            bank = psum.tile([P, 512], F32, name="bank")
-            for g in range(G):
+        def m_matmul(d, h):
+            rows, cols = slice(128 * d, 128 * d + 128), slice(512 * h, 512 * h + 512)
+            bank["m", d, h] = psum.tile([P, 512], F32, name="bank")
+            for g in range(GROUPS):
                 nc.tensor.matmul_mx(
-                    out=bank[:],
-                    lhsT=fc_codes[:, g, 128 * dt : 128 * dt + 128].bitcast(E4M3), lhsT_scale=fc_scales[:, g, 128 * dt : 128 * dt + 128],
-                    rhs=fp_codes[:, g, 512 * jh : 512 * jh + 512].bitcast(E4M3), rhs_scale=fp_scales[:, g, 512 * jh : 512 * jh + 512],
-                    start=(g == 0), stop=(g == 1),
+                    out=bank["m", d, h][:],
+                    lhsT=fc_codes[:, g, rows].bitcast(E4M3), lhsT_scale=fc_sc[:, g, rows],
+                    rhs=fp_codes[:, g, cols].bitcast(E4M3), rhs_scale=fp_sc[:, g, cols],
+                    start=(g == 0), stop=(g == GROUPS - 1),
                 )
-            banks["m", dt, jh] = bank
 
-        def product(dt, jh):
-            if dt not in t_R:
-                t_R[dt] = made(stage, [P, N], F32, "t_R", "k4", 4)
-            s = slice(512 * jh, 512 * jh + 512)
-            nc.vector.tensor_tensor(out=t_R[dt][:, s], in0=banks["m", dt, jh][:], in1=q_sb[:, dt, s], op=ALU.mult)
+        def product(d, h):
+            if d not in out_sb:
+                out_sb[d] = new(stage_pool, [P, N], F32, "out_sb", "row", 4)
+            cols = slice(512 * h, 512 * h + 512)
+            nc.vector.tensor_tensor(out=out_sb[d][:, cols], in0=bank["m", d, h][:], in1=q_sb[:, d, cols], op=ALU.mult)
 
-        def store_R(dt):
-            nc.sync.dma_start(out=out_0[128 * dt : 128 * dt + 128, :], in_=t_R[dt][:])
+        def store_out(d):
+            nc.sync.dma_start(out=out_0[128 * d : 128 * d + 128, :], in_=out_sb[d][:])
 
-        def round_R(dt, h):
-            if dt not in t_Rb:
-                t_Rb[dt] = made(stage, [P, 2, 2, P, 2], BF16, "t_Rb", None, 3)
-            src = t_R[dt][:, 512 * h : 512 * h + 512].rearrange("p (m u e) -> p u m e", u=2, e=2)
-            dst = t_Rb[dt][:, h]
-            if RND[dt][h] == "G":
-                nc.gpsimd.tensor_scalar(out=dst, in0=src, scalar1=1.0, scalar2=1.0, op0=ALU.mult, op1=ALU.mult)
-            elif RND[dt][h] == "V":
-                nc.vector.tensor_copy(out=dst, in_=src)
+        def round_half(engine, h, d):
+            if d not in out_bf:
+                out_bf[d] = new(stage_pool, [P, 2, 2, P, 2], BF16, "out_bf", None, 3)
+            src = out_sb[d][:, 512 * h : 512 * h + 512].rearrange("p (m u x) -> p u m x", u=2, x=2)
+            if engine == "gpsimd":
+                nc.gpsimd.tensor_scalar(
+                    out=out_bf[d][:, h], in0=src, scalar1=1.0, scalar2=1.0, op0=ALU.mult, op1=ALU.mult
+                )
             else:
-                nc.scalar.copy(out=dst, in_=src)
+                nc.scalar.copy(out=out_bf[d][:, h], in_=src)
 
-        def turn(dt, only=None):
-            if only != 1:
-                banks["t", dt] = psum_t.tile([P, 2, 2, P], F32, name="tbank")
-            bank = banks["t", dt]
-            words = t_Rb[dt][:].rearrange("p g u m e -> p (g u m e)").bitcast(F32)
-            for g in range(G) if only is None else (only,):
+        def turn(d, halves):
+            if halves[0] == 0:
+                bank["y", d] = psum_turn.tile([P, 2, 2, P], F32, name="turn_bank")
+            words = out_bf[d][:].rearrange("p h u m x -> p (h u m x)").bitcast(F32)
+            for h in halves:
                 for u in range(2):
-                    k = 2 * g + u
-                    nc.tensor.transpose(bank[:, g, u, :], words[:, 128 * k : 128 * k + 128], ident[:])
+                    w0 = 256 * h + 128 * u
+                    nc.tensor.transpose(bank["y", d][:, h, u, :], words[:, w0 : w0 + 128], ident[:])
 
-        def group(dt):
-            for i, (d0, d1) in enumerate(YG):
-                if d0 <= dt < d1:
-                    return i, d0, d1
-
-        def y_evac(dt, only=None):
-            i, d0, d1 = group(dt)
-            w = 128 * (d1 - d0)
-            if i not in t_y:
-                t_y[i] = made(keep, [P, G, w, 4], BF16, "t_y%d" % i, "big" if w <= 256 else None, 4 if w <= 256 else 1)
-            dst = t_y[i][:].rearrange("p g d t -> p (g d t)").bitcast(F32).rearrange("p (g d u) -> p g d u", g=G, u=2)
-            s = slice(128 * (dt - d0), 128 * (dt - d0) + 128)
-            src = banks["t", dt][:].rearrange("p g u d -> p g d u")
-            if only is None:
-                nc.scalar.copy(out=dst[:, :, s, :], in_=src)
+        def y_copy(d, halves):
+            i = y_set(d)
+            d0, d1 = Y_SETS[i]
+            if i not in y_il:
+                small = d1 - d0 <= 2
+                y_il[i] = new(keep, [P, 2, 128 * (d1 - d0), 4], BF16, "y_il%d" % i, "raw" if small else None, 4 if small else 1)
+            dst = y_il[i][:].rearrange("p h d t -> p (h d t)").bitcast(F32).rearrange("p (h d u) -> p h d u", h=2, u=2)
+            dst = dst[:, :, 128 * (d - d0) : 128 * (d - d0) + 128, :]
+            src = bank["y", d][:].rearrange("p h u d -> p h d u")
+            if len(halves) == 2:
+                nc.scalar.copy(out=dst, in_=src)
             else:
-                nc.scalar.copy(out=dst[:, only, s, :], in_=src[:, only])
+                nc.scalar.copy(out=dst[:, halves[0]], in_=src[:, halves[0]])
 
-        def y_quant(i, g):
-            d0, d1 = YG[i]
-            w = 128 * (d1 - d0)
+        def quantise_y(i, g):
+            d0, d1 = Y_SETS[i]
             if i not in y_codes:
-                y_codes[i] = made(keep, [P, G, w], U32, "y_codes%d" % i)
-            half = d0 // 4
-            if half not in y_scales:
-                y_scales[half] = made(keep, [P, G, 512], U8, "y_scales%d" % half)
-            s0 = 128 * (d0 % 4)
+                y_codes[i] = new(keep, [P, GROUPS, 128 * (d1 - d0)], U32, "y_codes%d" % i)
+            if d0 // 4 not in y_sc:
+                y_sc[d0 // 4] = new(keep, [P, GROUPS, 512], U8, "y_sc%d" % (d0 // 4))
             nc.vector.quantize_mx(
-                out=y_codes[i][:, g, :].bitcast(E4M3), scales=y_scales[half][:, g, s0 : s0 + w],
-                in_=t_y[i][:, g, :, :].rearrange("p d t -> p (d t)"),
+                out=y_codes[i][:, g, :].bitcast(E4M3),
+                scales=y_sc[d0 // 4][:, g, 128 * (d0 % 4) : 128 * (d0 % 4) + 128 * (d1 - d0)],
+                in_=y_il[i][:, g, :, :].rearrange("p d t -> p (d t)"),
             )
 
-        def y_store(i):
-            m0, m1 = 128 * YG[i][0], 128 * YG[i][1]
+        def store_codes(i):
+            m0, m1 = 128 * Y_SETS[i][0], 128 * Y_SETS[i][1]
             nc.sync.dma_start(
                 out=out_1[:, :, m0:m1, :].rearrange("g p m t -> p g (m t)").bitcast(I32), in_=y_codes[i][:].bitcast(I32)
             )
 
-        def s_store(i):
-            m0, m1 = 512 * i, 512 * i + 512
-            for Q in range(4):
+        def store_scales(half):
+            for quad in range(4):
                 nc.sync.dma_start(
-                    out=out_2[:, 4 * Q : 4 * Q + 4, m0:m1].rearrange("g q m -> q g m").bitcast(I32),
-                    in_=y_scales[i][32 * Q : 32 * Q + 4, :, :].bitcast(I32),
+                    out=out_2[:, 4 * quad : 4 * quad + 4, 512 * half : 512 * half + 512].rearrange("g s m -> s g m").bitcast(I32),
+                    in_=y_sc[half][32 * quad : 32 * quad + 4, :, :].bitcast(I32),
                 )
 
-        VEC = [("abs", 0), ("gv", 0, 0), ("fac",), ("gv", 1, 0), ("gq", 0, 0), ("fC",), ("gq", 1, 0), ("abs", 1), ("fc", 0), ("gv", 0, 1), ("fp", 0), ("gq", 0, 1), ("gv", 1, 1), ("abs", 2), ("qfp", 0), ("gq", 1, 1), ("qfc", 0), ("pq", 0, 2, 0), ("abs", 3), ("fp", 1), ("fp", 2), ("pq", 0, 2, 1), ("fp", 3), ("abs", 4), ("qfp", 1), ("qfp", 2), ("fp", 4), ("fc", 4), ("qfp", 3), ("qfc", 1), ("fp", 5), ("pq", 2, 4, 0), ("fp", 6), ("qfc", 4), ("qfp", 4), ("pq", 2, 4, 1), ("qfp", 5), ("qfc", 5), ("fp", 7), ("qfp", 6), ("qfp", 7), ("pr", 0, 0), ("pq", 4, 6, 1), ("pq", 4, 6, 0), ("pr", 0, 1), ("pr", 1, 0), ("pr", 1, 1), ("pr", 2, 0), ("fc", 2), ("fc", 6), ("qfc", 2), ("pq", 6, 8, 1), ("qfc", 6), ("pr", 2, 1), ("pq", 6, 8, 0), ("rfc", 7), ("pr", 3, 0), ("pr", 3, 1), ("fc", 3), ("pr", 4, 0), ("qfc", 3), ("qfc", 7), ("pr", 4, 1), ("pr", 5, 0), ("pr", 5, 1), ("pr", 6, 0), ("pr", 6, 1), ("yq", 0, 1), ("yq", 0, 0), ("pr", 7, 0), ("pr", 7, 1), ("yq", 1, 0), ("yq", 1, 1), ("yq", 2, 0), ("yq", 2, 1), ("yq", 3, 0), ("yq", 3, 1)]
-        SCA = [("gs", 0, 0), ("gs", 1, 0), ("cos", 0), ("pe", 0, 0), ("gs", 0, 1), ("gs", 1, 1), ("pe", 1, 0), ("cos", 1), ("cos", 2), ("cos", 3), ("pe", 0, 1), ("pe", 2, 0), ("pe", 1, 1), ("cos", 4), ("cos", 5), ("qe", 0, 0), ("pe", 3, 0), ("pe", 4, 0), ("cos", 6), ("pe", 2, 1), ("pe", 3, 1), ("pe", 4, 1), ("pe", 5, 1), ("qe", 0, 1), ("pe", 5, 0), ("cos", 7), ("pe", 6, 1), ("pe", 6, 0), ("qe", 1, 0), ("pe", 7, 0), ("qe", 1, 1), ("qe", 2, 0), ("qe", 2, 1), ("qe", 3, 0), ("pe", 7, 1), ("qe", 3, 1), ("qe", 4, 0), ("qe", 4, 1), ("y", 0), ("qe", 5, 0), ("wfc", 7), ("qe", 5, 1), ("y", 1), ("qe", 6, 0), ("y", 2), ("qe", 6, 1), ("qe", 7, 0), ("rd", 5, 1), ("y", 3), ("rd", 6, 1), ("y", 4), ("y", 5), ("qe", 7, 1), ("y", 6), ("rd", 7, 1), ("y", 7, 0), ("y", 7, 1)]
-        TEN = [("fT", 0), ("fT", 1), ("s1", 0, 0), ("s1", 1, 0), ("s1", 2, 0), ("s1", 0, 1), ("s1", 1, 1), ("s1", 3, 0), ("s1", 4, 0), ("s1", 2, 1), ("q", 0, 0), ("s1", 3, 1), ("s1", 4, 1), ("s1", 5, 1), ("s1", 5, 0), ("q", 0, 1), ("q", 1, 0), ("s1", 6, 1), ("s1", 6, 0), ("s1", 7, 0), ("s1", 7, 1), ("q", 1, 1), ("m", 0, 0), ("q", 2, 0), ("q", 2, 1), ("m", 0, 1), ("m", 1, 0), ("m", 1, 1), ("m", 2, 0), ("q", 3, 0), ("t", 0), ("q", 3, 1), ("q", 4, 0), ("q", 4, 1), ("q", 5, 0), ("m", 2, 1), ("q", 5, 1), ("m", 3, 0), ("m", 3, 1), ("m", 4, 0), ("m", 4, 1), ("m", 5, 0), ("t", 1), ("t", 2), ("q", 6, 0), ("q", 6, 1), ("m", 5, 1), ("q", 7, 0), ("m", 6, 0), ("m", 6, 1), ("t", 3), ("t", 4), ("m", 7, 0), ("t", 5), ("q", 7, 1), ("m", 7, 1), ("t", 6), ("t", 7, 0), ("t", 7, 1)]
-        GPS = [("fc", 1), ("fc", 5), ("rd", 0, 0), ("rd", 0, 1), ("rd", 1, 0), ("rd", 1, 1), ("rd", 2, 0), ("rd", 2, 1), ("rd", 3, 0), ("rd", 4, 0), ("rd", 3, 1), ("rd", 4, 1), ("rd", 5, 0), ("rd", 6, 0), ("rd", 7, 0)]
-        SYN = [("oR", 0), ("oR", 1), ("oR", 2), ("oR", 3), ("oR", 4), ("oy", 0), ("os", 0), ("oR", 5), ("oy", 1), ("oR", 6), ("oy", 2), ("oR", 7), ("oy", 3), ("os", 1)]
-        table = {
-            "abs": absolute, "cos": cosine, "fac": factors, "fT": factor_turn, "fC": factor_copy,
-            "gv": lambda gk, ge: gup_copy(gk, ge, "V"), "gs": lambda gk, ge: gup_copy(gk, ge, "S"), "gq": gup_quant,
-            "s1": stage1, "pe": p_evac, "pv": p_evac_v, "pq": p_quant, "q": q_mm, "qe": q_evac, "m": m_mm, "pr": product, "rd": round_R,
-            "t": turn, "y": y_evac, "yq": y_quant, "oR": store_R, "oy": y_store, "os": s_store,
-            "fp": lambda k: times("fp", k), "fc": lambda k: times("fc", k),
-            "qfp": lambda k: quant_f("fp", k), "qfc": lambda k: quant_f("fc", k),
-            "rfp": lambda k: rows("fp", k), "rfc": lambda k: rows("fc", k),
-            "wfp": lambda k: weave_rows("fp", k), "wfc": lambda k: weave_rows("fc", k),
+        put = {
+            "abs": absolute,
+            "sine": sine,
+            "factors": factors,
+            "fp": lambda i: times("fp", r_f, i),
+            "fc": lambda i: times("fc", cr_f, i),
+            "fp_q": lambda i: quantise_f("fp", fp_codes, fp_sc, i),
+            "fc_q": lambda i: quantise_f("fc", fc_codes, fc_sc, i),
+            "gup_lo": lambda k, e: interleave_gup("vector", k, e),
+            "gup_hi": lambda k, e: interleave_gup("scalar", k, e),
+            "gup_q": quantise_gup,
+            "p": p_matmul,
+            "p_copy": p_copy,
+            "p_q": quantise_p,
+            "q": q_matmul,
+            "q_copy": q_copy,
+            "m": m_matmul,
+            "product": product,
+            "round_lo": lambda d: round_half("gpsimd", 0, d),
+            "round_hi": lambda d: round_half("scalar", 1, d),
+            "turn": turn,
+            "y_copy": y_copy,
+            "y_q": quantise_y,
+            "store_out": store_out,
+            "store_codes": store_codes,
+            "store_scales": store_scales,
         }
-        widths = [x for x in VEC if x[0] == "pq"]
 
-        def needs(x):
-            n, v = x[0], x[1:]
-            if n == "cos":
-                return [("abs", a_tile(v[0])[0])]
-            if n in ("fp", "fc"):
-                return [("cos", v[0]), ("fT", 1) if PSUM_FACTORS and (n, v[0]) not in ON_G else ("fac",)]
-            if n in ("rfp", "rfc"):
-                return [("cos", v[0]), ("fac",)]
-            if n in ("wfp", "wfc"):
-                return [("r" + n[1:], v[0])]
-            if n in ("qfp", "qfc"):
-                return [("w" + n[1:], v[0]) if (n[1:], v[0]) in ON_S else (n[1:], v[0])]
-            if n == "fT":
-                return [("fac",)] if v[0] == 0 else [("fC",)]
-            if n == "fC":
-                return [("fT", 0)]
-            if n == "gq":
-                return [("gv",) + v, ("gs",) + v]
-            if n == "s1":
-                return [("gq", 0, v[1]), ("gq", 1, v[1])]
-            if n in ("pe", "pv"):
-                return [("s1",) + v]
-            if n == "pq":
-                return [("pe", d, v[2]) if ("pe", d, v[2]) in SCA else ("pv", d, v[2]) for d in range(v[0], v[1])]
-            if n == "q":
-                return [w for w in widths if w[1] <= v[0] < w[2]]
-            if n == "qe":
-                return [("q",) + v]
-            if n == "m":
-                return [("qfc", v[0] // 2), ("qfc", 4 + v[0] // 2)] + [("qfp", 4 * g + 2 * v[1] + h) for g in range(2) for h in range(2)]
-            if n == "pr":
-                return [("m",) + v, ("qe",) + v]
-            if n == "rd":
-                return [("pr",) + v]
-            if n == "t":
-                return [("rd", v[0], 0), ("rd", v[0], 1)] if len(v) == 1 else [("rd",) + v]
-            if n == "y":
-                return [("t",) + v]
-            if n == "yq":
-                return [("y", d) if ("y", d) in SCA else ("y", d, v[1]) for d in range(YG[v[0]][0], YG[v[0]][1])]
-            if n == "oR":
-                return [("pr", v[0], 0), ("pr", v[0], 1)]
-            if n == "oy":
-                return [("yq", v[0], 0), ("yq", v[0], 1)]
-            if n == "os":
-                return [("yq", i, g) for i in range(len(YG)) if YG[i][0] // 4 == v[0] for g in range(G)]
-            return []
-
-        queues = [list(VEC), list(SCA), list(TEN), list(GPS), list(SYN)]
+        queues = calls_of((VECTOR, SCALAR, TENSOR, GPSIMD, SYNC))
         seen = set()
         while any(queues):
-            moved = False
-            for qq in queues:
-                while qq and all(x in seen for x in needs(qq[0])):
-                    x = qq.pop(0)
-                    table[x[0]](*x[1:])
-                    seen.add(x)
-                    moved = True
-            assert moved, "no operation can go: %s" % [(qq[0], [x for x in needs(qq[0]) if x not in seen]) for qq in queues if qq]
+            before = len(seen)
+            for queue in queues:
+                while queue and all(call in seen for call in NEEDS.get(queue[0][0], lambda *x: [])(*queue[0][1:])):
+                    call = queue.pop(0)
+                    put[call[0]](*call[1:])
+                    seen.add(call)
+            assert len(seen) > before, "the engines' orders contradict each other"

from contextlib import ExitStack

import math

import concourse.mybir as mybir
from concourse.masks import make_identity

F32 = mybir.dt.float32
BF16 = mybir.dt.bfloat16
U32 = mybir.dt.uint32
I32 = mybir.dt.int32
U8 = mybir.dt.uint8
E4M3 = mybir.dt.float8_e4m3fn_x4
E2M1 = mybir.dt.float4_e2m1fn_x4
ALU = mybir.AluOpType
ACT = mybir.ActivationFunctionType

P = 128
N = 1024
GROUPS = 2
TILES = 8
CHUNK = 256
CHUNKS = 8
FLOPS = 3 * 2 * N * N * N

A_PARTS = ((0, 0, 256), (0, 256, 512), (0, 512, 1024), (1, 0, 512), (1, 512, 1024))

Y_SETS = ((0, 4), (4, 6), (6, 7), (7, 8))

VECTOR = """
abs gup_lo fc fp gup_lo abs gup_q*2 gup_lo fc gup_q gup_lo abs gup_q fp abs p_q fp_q fp*3 fc_q fc p_q fc abs
fp p_q*2 fc_q fp_q*2 fp*2 p_q fp_q product fc product*2 p_q fc product*2 fc product fc fc_q*2 product*3
p_q*2 product*3 y_q*2 product*3 y_q*2 product y_q*4
"""
SCALAR = """
sine gup_hi*2 sine gup_hi*2 p_copy*2 sine*4 p_copy*8 q_copy p_copy q_copy sine*2 p_copy*2 q_copy*2 p_copy
q_copy*3 round_hi p_copy y_copy round_hi q_copy*2 round_hi q_copy*2 p_copy y_copy*2 round_hi q_copy y_copy
round_hi q_copy round_hi q_copy*2 y_copy*2 round_hi q_copy y_copy round_hi y_copy*2
"""
TENSOR = """
p*11 q*4 p*3 m q*3 p m*5 turn q*3 m q p m turn*2 q m*4 turn m q*2 m q turn*2 m q m turn*3
"""
GPSIMD = "factors round_lo*8"
SYNC = "store_out*5 store_codes store_scales store_out store_codes store_out store_codes store_out store_codes store_scales"

PAIRS = [(a, b) for a in range(TILES) for b in range(2)]
GUP_PARTS = [(0, 0), (1, 0), (0, 1), (1, 1)]
P_PARTS = [(0, 0)] + [(d + 1 - g, g) for d in range(TILES - 1) for g in range(2)] + [(TILES - 1, 1)]
FC_CHUNKS = [(0,), (1,), (4,), (5,), (2,), (3,), (6,), (7,)]
TURNS = [(d, (0, 1)) for d in range(TILES - 1)] + [(TILES - 1, (0,)), (TILES - 1, (1,))]

STREAMS = {
    "abs": [(i,) for i in range(len(A_PARTS))],
    "sine": [(i,) for i in range(CHUNKS)],
    "factors": [()],
    "fp": [(i,) for i in range(CHUNKS)],
    "fc": FC_CHUNKS,
    "fp_q": [(i,) for i in range(0, CHUNKS, 2)],
    "fc_q": FC_CHUNKS[::2],
    "gup_lo": GUP_PARTS,
    "gup_hi": GUP_PARTS,
    "gup_q": GUP_PARTS,
    "p": P_PARTS,
    "p_copy": P_PARTS,
    "p_q": [(d, g) for d in range(0, TILES, 2) for g in range(GROUPS)],
    "q": PAIRS,
    "q_copy": PAIRS,
    "m": PAIRS,
    "product": PAIRS,
    "round_lo": [(d,) for d in range(TILES)],
    "round_hi": [(d,) for d in range(TILES)],
    "turn": TURNS,
    "y_copy": TURNS,
    "y_q": [(i, g) for i in range(len(Y_SETS)) for g in range(GROUPS)],
    "store_out": [(d,) for d in range(TILES)],
    "store_codes": [(i,) for i in range(len(Y_SETS))],
    "store_scales": [(h,) for h in range(2)],
}


def a_part(chunk):
    group, col = chunk // 4, CHUNK * (chunk % 4)
    for i, (g, c0, c1) in enumerate(A_PARTS):
        if g == group and c0 <= col < c1:
            return i, col - c0


def y_set(tile):
    return [i for i, (d0, d1) in enumerate(Y_SETS) if d0 <= tile < d1][0]


NEEDS = {
    "sine": lambda i: [("abs", a_part(i)[0])],
    "fp": lambda i: [("sine", i), ("factors",)],
    "fc": lambda i: [("sine", i), ("factors",)],
    "fp_q": lambda i: [("fp", i), ("fp", i + 1)],
    "fc_q": lambda i: [("fc", i), ("fc", i + 1)],
    "gup_q": lambda k, e: [("gup_lo", k, e), ("gup_hi", k, e)],
    "p": lambda d, e: [("gup_q", 0, e), ("gup_q", 1, e)],
    "p_copy": lambda d, e: [("p", d, e)],
    "p_q": lambda d, e: [("p_copy", d, e), ("p_copy", d + 1, e)],
    "q": lambda d, h: [("p_q", d // 2 * 2, e) for e in range(GROUPS)],
    "q_copy": lambda d, h: [("q", d, h)],
    "m": lambda d, h: [(s, 4 * g + 2 * c) for g in range(GROUPS) for s, c in (("fc_q", d // 4), ("fp_q", h))],
    "product": lambda d, h: [("m", d, h), ("q_copy", d, h)],
    "round_lo": lambda d: [("product", d, 0)],
    "round_hi": lambda d: [("product", d, 1)],
    "turn": lambda d, halves: [(("round_lo", "round_hi")[h], d) for h in halves],
    "y_copy": lambda d, halves: [("turn", d, halves)],
    "y_q": lambda i, g: [("y_copy",) + t for t in TURNS if y_set(t[0]) == i and g in t[1]],
    "store_out": lambda d: [("product", d, 0), ("product", d, 1)],
    "store_codes": lambda i: [("y_q", i, g) for g in range(GROUPS)],
    "store_scales": lambda h: [("y_q", i, g) for i in range(len(Y_SETS)) if Y_SETS[i][0] // 4 == h for g in range(GROUPS)],
}


def calls_of(orders):
    streams = {stage: list(calls) for stage, calls in STREAMS.items()}
    lists = []
    for order in orders:
        calls = []
        for run in order.split():
            stage, count = (run.split("*") + ["1"])[:2]
            for i in range(int(count)):
                calls.append((stage,) + streams[stage].pop(0))
        lists.append(calls)
    return lists


def tile_kfrasinecurvaturepullback_x2_kernel(tc, w_words, w_scales, gup, a, r, c, out_0, out_1, out_2):
    nc = tc.nc
    with ExitStack() as ctx:
        keep = ctx.enter_context(tc.tile_pool(name="keep", bufs=1))
        stage_pool = ctx.enter_context(tc.tile_pool(name="stage", bufs=3))
        psum = ctx.enter_context(tc.psum_pool(name="psum", bufs=6))
        psum_turn = ctx.enter_context(tc.psum_pool(name="psum_turn", bufs=2))
        ctx.enter_context(tc.manual_schedule())

        def new(pool, shape, dtype, name, tag=None, bufs=1):
            return pool.tile(shape, dtype, align_bytes=64, name=name, tag=tag or name, bufs=bufs)

        a_sb = []
        for i, (g, c0, c1) in enumerate(A_PARTS):
            a_sb.append(new(keep, [P, 4, c1 - c0], BF16, "a%d" % i))
        gup_sb = {}
        for k, e in GUP_PARTS:
            gup_sb[k, e] = new(keep, [P, 4, 512], BF16, "gup%d%d" % (k, e), "raw", 4)
        w_sb = new(keep, [P, GROUPS, 2 * N], U8, "w_sb")
        w_sc = new(keep, [P, GROUPS, N], U8, "w_sc")
        r_bf = new(keep, [P, 4 * GROUPS], BF16, "r_bf")
        c_bf = new(keep, [P, 4 * GROUPS], BF16, "c_bf")
        ident = new(keep, [P, P], F32, "ident")
        r_f = new(keep, [P, 4 * GROUPS], F32, "r_f")
        cr_f = new(keep, [P, 4 * GROUPS], F32, "cr_f")
        gup_codes = new(keep, [P, GROUPS, N], U32, "gup_codes")
        gup_sc = new(keep, [P, GROUPS, N], U8, "gup_sc")
        fp_codes = new(keep, [P, GROUPS, N], U32, "fp_codes")
        fp_sc = new(keep, [P, GROUPS, N], U8, "fp_sc")
        fc_codes = new(keep, [P, GROUPS, N], U32, "fc_codes")
        fc_sc = new(keep, [P, GROUPS, N], U8, "fc_sc")
        cos_sb = new(keep, [P, CHUNKS, 4, CHUNK], F32, "cos_sb")
        p_bf = new(keep, [P, GROUPS, N, 4], BF16, "p_bf")
        p_codes = new(keep, [P, GROUPS, N], U32, "p_codes")
        p_sc = new(keep, [P, GROUPS, N], U8, "p_sc")
        q_sb = new(keep, [P, TILES, N], F32, "q_sb")
        a_abs, gup_il, f_il, bank, out_sb, out_bf, y_il, y_codes, y_sc = {}, {}, {}, {}, {}, {}, {}, {}, {}

        def load_a(i):
            g, c0, c1 = A_PARTS[i]
            nc.sync.dma_start(out=a_sb[i][:], in_=a[512 * g : 512 * g + 512, c0:c1].rearrange("(p t) i -> p t i", t=4))

        def load_gup(k, e):
            rows, cols = slice(512 * k, 512 * k + 512), slice(512 * e, 512 * e + 512)
            nc.sync.dma_start(out=gup_sb[k, e][:], in_=gup[rows, cols].rearrange("(p t) e -> p t e", t=4))

        nc.vector.memset(w_sc[:].rearrange("p g n -> p (g n)").bitcast(I32), 0)
        make_identity(nc, ident[:])
        load_a(0)
        load_gup(0, 0)
        for vec, tile in ((r, r_bf), (c, c_bf)):
            nc.sync.dma_start(
                out=tile[:].rearrange("p (g t) -> p g t", g=GROUPS), in_=vec.rearrange("(g p t) -> p g t", g=GROUPS, t=4)
            )
        load_gup(1, 0)
        nc.sync.dma_start(out=w_sb[:].bitcast(I32), in_=w_words.rearrange("g p n -> p g n").bitcast(I32))
        for quad in range(4):
            nc.sync.dma_start(
                out=w_sc[32 * quad : 32 * quad + 4, :, :].bitcast(I32),
                in_=w_scales[:, 4 * quad : 4 * quad + 4, :].rearrange("g s n -> s g n").bitcast(I32),
            )
        load_a(1)
        load_gup(0, 1)
        load_gup(1, 1)
        load_a(2)
        load_a(3)
        load_a(4)

        def absolute(i):
            width = A_PARTS[i][2] - A_PARTS[i][1]
            a_abs[i] = new(stage_pool, [P, 4, width], BF16, "a_abs", None, 3)
            nc.vector.tensor_scalar(
                out=a_abs[i][:].rearrange("p t i -> p (t i)").bitcast(I32),
                in0=a_sb[i][:].rearrange("p t i -> p (t i)").bitcast(I32),
                scalar1=0x7FFF7FFF, scalar2=None, op0=ALU.bitwise_and,
            )

        def sine(i):
            part, c0 = a_part(i)
            nc.scalar.activation(
                out=cos_sb[:, i], in_=a_abs[part][:, :, c0 : c0 + CHUNK], func=ACT.Sin, scale=-1.0, bias=math.pi / 2
            )

        def factors():
            nc.gpsimd.tensor_copy(out=r_f[:], in_=r_bf[:])
            nc.gpsimd.tensor_tensor(out=cr_f[:], in0=c_bf[:], in1=r_bf[:], op=ALU.mult)

        def times(name, factor, i):
            if (name, i // 2) not in f_il:
                f_il[name, i // 2] = new(stage_pool, [P, 2 * CHUNK, 4], BF16, "f_il", None, 3)
            half = slice(CHUNK * (i % 2), CHUNK * (i % 2) + CHUNK)
            g = i // 4
            nc.vector.tensor_tensor(
                out=f_il[name, i // 2][:, half, :].rearrange("p (c i) t -> p c t i", i=4),
                in0=cos_sb[:, i].rearrange("p t (c i) -> p c t i", i=4),
                in1=factor[:, 4 * g : 4 * g + 4].unsqueeze(1).unsqueeze(3).broadcast_to([P, CHUNK // 4, 4, 4]),
                op=ALU.mult,
            )

        def quantise_f(name, codes, scales, i):
            g, cols = i // 4, slice(CHUNK * (i % 4), CHUNK * (i % 4) + 2 * CHUNK)
            nc.vector.quantize_mx(
                out=codes[:, g, cols].bitcast(E4M3), scales=scales[:, g, cols],
                in_=f_il[name, i // 2][:].rearrange("p i t -> p (i t)"),
            )

        def interleave_gup(engine, k, e):
            if (k, e) not in gup_il:
                gup_il[k, e] = new(stage_pool, [P, 4, P, 4], BF16, "gup_il", "row", 4)
            t = slice(0, 2) if engine == "vector" else slice(2, 4)
            src = gup_sb[k, e][:].rearrange("p j (m t) -> p t m j", t=4)
            if engine == "vector":
                nc.vector.tensor_copy(out=gup_il[k, e][:, t], in_=src[:, t])
            else:
                nc.scalar.copy(out=gup_il[k, e][:, t], in_=src[:, t])

        def quantise_gup(k, e):
            cols = slice(512 * e, 512 * e + 512)
            nc.vector.quantize_mx(
                out=gup_codes[:, k, cols].bitcast(E4M3), scales=gup_sc[:, k, cols],
                in_=gup_il[k, e][:].rearrange("p t m j -> p (t m j)"),
            )

        def p_matmul(d, e):
            bank["p", d, e] = psum.tile([P, 512], F32, name="bank")
            for t in range(4):
                cols = slice(512 * e + 128 * t, 512 * e + 128 * t + 128)
                for k in range(GROUPS):
                    nc.tensor.matmul_mx(
                        out=bank["p", d, e][:, 128 * t : 128 * t + 128],
                        lhsT=gup_codes[:, k, cols].bitcast(E4M3), lhsT_scale=gup_sc[:, k, cols],
                        rhs=w_sb[:, k, 256 * d : 256 * d + 256].bitcast(E2M1), rhs_scale=w_sc[:, k, 128 * d : 128 * d + 128],
                        start=(k == 0), stop=(k == GROUPS - 1),
                    )

        def p_copy(d, e):
            nc.scalar.copy(
                out=p_bf[:, e, 128 * d : 128 * d + 128, :], in_=bank["p", d, e][:].rearrange("p (t d) -> p d t", t=4)
            )

        def quantise_p(d, e):
            rows = slice(128 * d, 128 * d + 256)
            nc.vector.quantize_mx(
                out=p_codes[:, e, rows].bitcast(E4M3), scales=p_sc[:, e, rows],
                in_=p_bf[:, e, rows, :].rearrange("p d t -> p (d t)"),
            )

        def q_matmul(d, h):
            rows, cols = slice(128 * d, 128 * d + 128), slice(512 * h, 512 * h + 512)
            bank["q", d, h] = psum.tile([P, 512], F32, name="bank")
            for e in range(GROUPS):
                nc.tensor.matmul_mx(
                    out=bank["q", d, h][:],
                    lhsT=p_codes[:, e, rows].bitcast(E4M3), lhsT_scale=p_sc[:, e, rows],
                    rhs=w_sb[:, e, 1024 * h : 1024 * h + 1024].bitcast(E2M1), rhs_scale=w_sc[:, e, cols],
                    start=(e == 0), stop=(e == GROUPS - 1),
                )

        def q_copy(d, h):
            nc.scalar.activation(
                out=q_sb[:, d, 512 * h : 512 * h + 512], in_=bank["q", d, h][:], func=ACT.Copy, scale=1.0 / N
            )

        def m_matmul(d, h):
            rows, cols = slice(128 * d, 128 * d + 128), slice(512 * h, 512 * h + 512)
            bank["m", d, h] = psum.tile([P, 512], F32, name="bank")
            for g in range(GROUPS):
                nc.tensor.matmul_mx(
                    out=bank["m", d, h][:],
                    lhsT=fc_codes[:, g, rows].bitcast(E4M3), lhsT_scale=fc_sc[:, g, rows],
                    rhs=fp_codes[:, g, cols].bitcast(E4M3), rhs_scale=fp_sc[:, g, cols],
                    start=(g == 0), stop=(g == GROUPS - 1),
                )

        def product(d, h):
            if d not in out_sb:
                out_sb[d] = new(stage_pool, [P, N], F32, "out_sb", "row", 4)
            cols = slice(512 * h, 512 * h + 512)
            nc.vector.tensor_tensor(out=out_sb[d][:, cols], in0=bank["m", d, h][:], in1=q_sb[:, d, cols], op=ALU.mult)

        def store_out(d):
            nc.sync.dma_start(out=out_0[128 * d : 128 * d + 128, :], in_=out_sb[d][:])

        def round_half(engine, h, d):
            if d not in out_bf:
                out_bf[d] = new(stage_pool, [P, 2, 2, P, 2], BF16, "out_bf", None, 3)
            src = out_sb[d][:, 512 * h : 512 * h + 512].rearrange("p (m u x) -> p u m x", u=2, x=2)
            if engine == "gpsimd":
                nc.gpsimd.tensor_scalar(
                    out=out_bf[d][:, h], in0=src, scalar1=1.0, scalar2=1.0, op0=ALU.mult, op1=ALU.mult
                )
            else:
                nc.scalar.copy(out=out_bf[d][:, h], in_=src)

        def turn(d, halves):
            if halves[0] == 0:
                bank["y", d] = psum_turn.tile([P, 2, 2, P], F32, name="turn_bank")
            words = out_bf[d][:].rearrange("p h u m x -> p (h u m x)").bitcast(F32)
            for h in halves:
                for u in range(2):
                    w0 = 256 * h + 128 * u
                    nc.tensor.transpose(bank["y", d][:, h, u, :], words[:, w0 : w0 + 128], ident[:])

        def y_copy(d, halves):
            i = y_set(d)
            d0, d1 = Y_SETS[i]
            if i not in y_il:
                small = d1 - d0 <= 2
                y_il[i] = new(keep, [P, 2, 128 * (d1 - d0), 4], BF16, "y_il%d" % i, "raw" if small else None, 4 if small else 1)
            dst = y_il[i][:].rearrange("p h d t -> p (h d t)").bitcast(F32).rearrange("p (h d u) -> p h d u", h=2, u=2)
            dst = dst[:, :, 128 * (d - d0) : 128 * (d - d0) + 128, :]
            src = bank["y", d][:].rearrange("p h u d -> p h d u")
            if len(halves) == 2:
                nc.scalar.copy(out=dst, in_=src)
            else:
                nc.scalar.copy(out=dst[:, halves[0]], in_=src[:, halves[0]])

        def quantise_y(i, g):
            d0, d1 = Y_SETS[i]
            if i not in y_codes:
                y_codes[i] = new(keep, [P, GROUPS, 128 * (d1 - d0)], U32, "y_codes%d" % i)
            if d0 // 4 not in y_sc:
                y_sc[d0 // 4] = new(keep, [P, GROUPS, 512], U8, "y_sc%d" % (d0 // 4))
            nc.vector.quantize_mx(
                out=y_codes[i][:, g, :].bitcast(E4M3),
                scales=y_sc[d0 // 4][:, g, 128 * (d0 % 4) : 128 * (d0 % 4) + 128 * (d1 - d0)],
                in_=y_il[i][:, g, :, :].rearrange("p d t -> p (d t)"),
            )

        def store_codes(i):
            m0, m1 = 128 * Y_SETS[i][0], 128 * Y_SETS[i][1]
            nc.sync.dma_start(
                out=out_1[:, :, m0:m1, :].rearrange("g p m t -> p g (m t)").bitcast(I32), in_=y_codes[i][:].bitcast(I32)
            )

        def store_scales(half):
            for quad in range(4):
                nc.sync.dma_start(
                    out=out_2[:, 4 * quad : 4 * quad + 4, 512 * half : 512 * half + 512].rearrange("g s m -> s g m").bitcast(I32),
                    in_=y_sc[half][32 * quad : 32 * quad + 4, :, :].bitcast(I32),
                )

        put = {
            "abs": absolute,
            "sine": sine,
            "factors": factors,
            "fp": lambda i: times("fp", r_f, i),
            "fc": lambda i: times("fc", cr_f, i),
            "fp_q": lambda i: quantise_f("fp", fp_codes, fp_sc, i),
            "fc_q": lambda i: quantise_f("fc", fc_codes, fc_sc, i),
            "gup_lo": lambda k, e: interleave_gup("vector", k, e),
            "gup_hi": lambda k, e: interleave_gup("scalar", k, e),
            "gup_q": quantise_gup,
            "p": p_matmul,
            "p_copy": p_copy,
            "p_q": quantise_p,
            "q": q_matmul,
            "q_copy": q_copy,
            "m": m_matmul,
            "product": product,
            "round_lo": lambda d: round_half("gpsimd", 0, d),
            "round_hi": lambda d: round_half("scalar", 1, d),
            "turn": turn,
            "y_copy": y_copy,
            "y_q": quantise_y,
            "store_out": store_out,
            "store_codes": store_codes,
            "store_scales": store_scales,
        }

        queues = calls_of((VECTOR, SCALAR, TENSOR, GPSIMD, SYNC))
        seen = set()
        while any(queues):
            before = len(seen)
            for queue in queues:
                while queue and all(call in seen for call in NEEDS.get(queue[0][0], lambda *x: [])(*queue[0][1:])):
                    call = queue.pop(0)
                    put[call[0]](*call[1:])
                    seen.add(call)
            assert len(seen) > before, "the engines' orders contradict each other"
